import numpy as np
import ml_dtypes


def mxq(x, axis, fmt="e4m3"):
    dtype, down = {"e4m3": (ml_dtypes.float8_e4m3fn, 7), "e5m2": (ml_dtypes.float8_e5m2, 14)}[fmt]
    v = np.moveaxis(np.asarray(x, np.float32).astype(ml_dtypes.bfloat16).astype(np.float64), axis, -1)
    blocks = v.reshape(v.shape[:-1] + (-1, 32))
    amax = np.abs(blocks).max(-1, keepdims=True)
    byte = np.maximum(np.where(amax > 0, np.frexp(amax)[1] - 1 + 127, 0) - down, 1)
    scale = np.exp2(byte - 127.0)
    codes = (blocks / scale).astype(np.float32).astype(dtype).astype(np.float64)
    return np.moveaxis((codes * scale).reshape(v.shape), -1, axis)


WIDE = False


def mx_kscale(k):
    if not WIDE:
        return np.ones(k)
    levels = np.array([10, -10, 5, -5, 0])
    if k % 512:
        return np.exp2(np.random.permutation(np.resize(levels, k // 32))).repeat(32)
    a = np.empty((k // 512, 16))
    for p in range(k // 512):
        a[p, :8] = np.random.permutation(np.resize(levels, 8))
        for g in range(8):
            far = levels[np.abs(levels - a[p, g]) >= 10]
            a[p, g + 8] = far[np.random.randint(len(far))]
    return np.exp2(a.ravel()).repeat(32)


def f64(x):
    return np.asarray(x).astype(np.float64)


def striped(idx):
    return np.tile(idx.reshape(-1, 16).T, (8, 1)).astype(np.uint16)


def unstriped(offs):
    return offs[:16].T.reshape(-1).astype(np.int64)


K, T, E, C, N = 1536, 768, 6, 256, 128


def by_expert(wq, xq):
    return np.concatenate([wq[e].T @ xq[:, e * C:(e + 1) * C] for e in range(E)], axis=1)


def setup_inputs():
    n = np.random.standard_normal
    s = mx_kscale(K)[:, None]
    first = np.random.permutation(np.repeat(np.arange(E), T // E))
    second = (first + 1 + np.random.permutation(np.repeat(np.arange(E - 1), -(-T // (E - 1)))[:T])) % E
    while np.bincount(second, minlength=E).max() != T // E:
        load = np.bincount(second, minlength=E); hi, lo = int(load.argmax()), int(load.argmin())
        t = np.flatnonzero((second == hi) & (first != lo))[0]; second[t] = lo
    slot_token = np.empty(E * C, np.int64); pos = np.empty((2, T), np.int64); fill = np.zeros(E, np.int64)
    place = np.stack([np.random.permutation(C) for _ in range(E)])
    for r, deal in enumerate((first, second)):
        for t in np.random.permutation(T):
            e = deal[t]; j = e * C + place[e, fill[e]]; fill[e] += 1; slot_token[j] = t; pos[r, t] = j
    g = np.random.uniform(0.2, 0.8, T)
    w_slot = np.empty(E * C); w_slot[pos[0]] = g; w_slot[pos[1]] = 1.0 - g
    return {
        "xT": (n((K, T)) * s).astype(np.float32),
        "w": (n((E, K, N)) / np.sqrt(K) / s[None]).astype(np.float32),
        "b": (0.3 * n((N, E))).astype(np.float32),
        "gate": np.tile(w_slot, (K, 1)).astype(np.float32),
        "offs": striped(slot_token),
        "pos1": striped(pos[0]),
        "pos2": striped(pos[1]),
    }


def reference(xT, w, b, gate, offs, pos1, pos2):
    idx = unstriped(offs)
    xq = mxq(f64(gate) * f64(xT)[:, idx], 0, "e4m3")
    y = by_expert(mxq(f64(w), 1, "e4m3"), xq)
    y = y + np.repeat(f64(b), C, axis=1)
    return y[:, unstriped(pos1)] + y[:, unstriped(pos2)]

@@ -1,0 +1,179 @@
+from contextlib import ExitStack
+
+import concourse.mybir as mybir
+
+K, T, E, C, N = 1536, 768, 6, 256, 128
+S = E * C
+P = 128
+PACK = 4
+K_PASS = P * PACK
+PASSES = K // K_PASS
+PER_COL = 16
+
+FLOPS = 2 * K * S * N
+BYTES = 4 * (K * T + E * K * N + N * E + S + N * T) + 2 * P * (S + 2 * T) // PER_COL
+
+F32 = mybir.dt.float32
+BF16 = mybir.dt.bfloat16
+U32 = mybir.dt.uint32
+U16 = mybir.dt.uint16
+U8 = mybir.dt.uint8
+FP8X4 = mybir.dt.float8_e4m3fn_x4
+MULT = mybir.AluOpType.mult
+ADD = mybir.AluOpType.add
+IDENT = mybir.ActivationFunctionType.Identity
+
+CHUNK = 512
+GROUPS = [(0, 256), (256, 512), (512, 768), (768, 1024), (1024, 1280), (1280, 1408), (1408, 1536)]
+WIDE = [(0, 512), (512, 1024), (1024, 1536)]
+OUT = [(0, 384), (384, 576), (576, 768)]
+TAPER = [(0, 512), (512, 1024), (1024, 1280), (1280, 1408), (1408, 1536)]
+
+
+def interleave(nc, dst, src):
+    nc.scalar.copy(
+        out=dst.rearrange("p (c i) t -> p c t i", i=PACK),
+        in_=src.rearrange("p t (c i) -> p c t i", i=PACK),
+    )
+
+
+def tile_moe_pre_lin_bias_kernel(tc, xT, w, b, gate, offs, pos1, pos2, out):
+    nc = tc.nc
+    with ExitStack() as ctx:
+        keep = ctx.enter_context(tc.tile_pool(name="keep", bufs=1))
+        ring = ctx.enter_context(tc.tile_pool(name="ring", bufs=4))
+        psum = ctx.enter_context(tc.psum_pool(name="psum", bufs=1))
+
+        offs_sb = keep.tile([P, S // PER_COL], U16, name="offs_sb")
+        pos1_sb = keep.tile([P, T // PER_COL], U16, name="pos1_sb")
+        pos2_sb = keep.tile([P, T // PER_COL], U16, name="pos2_sb")
+        b_sb = keep.tile([P, E], F32, name="b_sb")
+        gate_sb = keep.tile([P, S], F32, name="gate_sb")
+        win = [[keep.tile([P, T], F32, name=f"win{g}{t}") for t in range(PACK)] for g in range(PASSES)]
+        w_raw = [keep.tile([P, E, PACK, N], F32, name=f"w_raw{g}") for g in range(PASSES)]
+        w_bf = [keep.tile([P, E, N, PACK], BF16, name=f"w_bf{g}", align_bytes=64) for g in range(PASSES)]
+        w_codes = [keep.tile([P, E * N], U32, name=f"w_codes{g}", align_bytes=64) for g in range(PASSES)]
+        w_scales = [keep.tile([P, E * N], U8, name=f"w_scales{g}", align_bytes=64) for g in range(PASSES)]
+        x_codes = [keep.tile([P, S], U32, name=f"x_codes{g}", align_bytes=64) for g in range(PASSES)]
+        x_scales = [keep.tile([P, S], U8, name=f"x_scales{g}", align_bytes=64) for g in range(PASSES)]
+        y = keep.tile([P, S], F32, name="y")
+        acc = [psum.tile([P, hi - lo], F32, name=f"acc{i}") for i, (lo, hi) in enumerate(GROUPS)]
+
+        x_rows = xT.rearrange("(g p t) x -> g t p x", g=PASSES, t=PACK)
+        w_rows = w.rearrange("e (g p t) n -> g p e t n", g=PASSES, t=PACK)
+
+        def load_gate(lo, hi):
+            nc.sync.dma_start(gate_sb[:, lo:hi], gate[0:P, lo:hi])
+
+        nc.sync.dma_start(offs_sb[:], offs)
+        nc.sync.dma_start(win[0][0][:], x_rows[0, 0])
+        load_gate(0, 256)
+        load_gate(256, 512)
+        for t in range(1, PACK):
+            nc.sync.dma_start(win[0][t][:], x_rows[0, t])
+        load_gate(*WIDE[1])
+        load_gate(*WIDE[2])
+        for g in range(PASSES):
+            nc.sync.dma_start(w_raw[g][:], w_rows[g])
+            if g + 1 < PASSES:
+                for t in range(PACK):
+                    nc.sync.dma_start(win[g + 1][t][:], x_rows[g + 1, t])
+        nc.sync.dma_start(b_sb[:], b)
+        nc.sync.dma_start(pos1_sb[:], pos1)
+        nc.sync.dma_start(pos2_sb[:], pos2)
+
+        def gather(g, lo, hi):
+            picked = ring.tile([P, PACK, CHUNK], F32, name="picked")
+            rounded = ring.tile([P, CHUNK, PACK], BF16, name="rounded", align_bytes=64)
+            n = hi - lo
+            for t in range(PACK):
+                cuts = [lo, 256, hi] if (g, t, lo) == (0, 0, 0) else [lo, hi]
+                for a, z in zip(cuts, cuts[1:]):
+                    nc.vector.tensor_tensor(
+                        picked[:, t, a - lo : z - lo],
+                        win[g][t][:].indirect(offs_sb[:, a // PER_COL : z // PER_COL]),
+                        gate_sb[:, a:z],
+                        MULT,
+                    )
+            interleave(nc, rounded[:, 0:n, :], picked[:, :, 0:n])
+            return rounded
+
+        def quantize_x(g, lo, hi, rounded):
+            nc.vector.quantize_mx(
+                out=x_codes[g][:, lo:hi].bitcast(FP8X4),
+                scales=x_scales[g][:, lo:hi],
+                in_=rounded[:, 0 : hi - lo, :].rearrange("p s t -> p (s t)"),
+            )
+
+        def round_w(g):
+            for e in range(E):
+                interleave(nc, w_bf[g][:, e], w_raw[g][:, e])
+
+        def quantize_w(g):
+            for e0, e1 in ((0, 4), (4, 6)):
+                nc.vector.quantize_mx(
+                    out=w_codes[g][:, e0 * N : e1 * N].bitcast(FP8X4),
+                    scales=w_scales[g][:, e0 * N : e1 * N],
+                    in_=w_bf[g][:, e0:e1].rearrange("p e n t -> p (e n t)"),
+                )
+
+        def multiply(g, lo, hi):
+            for i, (a, z) in enumerate(GROUPS):
+                if lo <= a and z <= hi:
+                    e = a // C
+                    nc.tensor.matmul_mx(
+                        out=acc[i][:],
+                        lhsT=w_codes[g][:, e * N : (e + 1) * N].bitcast(FP8X4),
+                        lhsT_scale=w_scales[g][:, e * N : (e + 1) * N],
+                        rhs=x_codes[g][:, a:z].bitcast(FP8X4),
+                        rhs_scale=x_scales[g][:, a:z],
+                        start=(g == 0),
+                        stop=(g == PASSES - 1),
+                    )
+                    if g == PASSES - 1:
+                        nc.scalar.activation(y[:, a:z], acc[i][:], IDENT, bias=b_sb[:, e : e + 1])
+
+        steps = [(g, lo, hi) for g in range(PASSES) for lo, hi in (TAPER if g == PASSES - 1 else WIDE)]
+        w_round_at = {1: 0, 3: 1, 5: 2}
+        w_quant_at = {2: 0, 4: 1, 6: 2}
+        done_w = set()
+        waiting = []
+        previous = None
+        for i, step in enumerate(steps + [None]):
+            current = None
+            if step is not None:
+                current = (step, gather(*step))
+            if i in w_round_at:
+                round_w(w_round_at[i])
+            if previous is not None:
+                quantize_x(*previous[0], previous[1])
+                waiting.append(previous[0])
+            if i in w_quant_at:
+                quantize_w(w_quant_at[i])
+                done_w.add(w_quant_at[i])
+            for s in list(waiting):
+                if s[0] in done_w:
+                    multiply(*s)
+                    waiting.remove(s)
+            previous = current
+
+        first = keep.tile([P, T], F32, name="first")
+        second = [keep.tile([P, hi - lo], F32, name=f"second{lo}") for lo, hi in OUT]
+        total = [keep.tile([P, hi - lo], F32, name=f"total{lo}") for lo, hi in OUT]
+
+        def fetch(i):
+            lo, hi = OUT[i]
+            nc.vector.tensor_copy(second[i][:], y[:].indirect(pos2_sb[:, lo // PER_COL : hi // PER_COL]))
+
+        def combine(i):
+            lo, hi = OUT[i]
+            nc.vector.tensor_tensor(total[i][:], first[:, lo:hi], second[i][:], ADD)
+            queue = nc.scalar if i % 2 else nc.sync
+            queue.dma_start(out[:, lo:hi], total[i][:])
+
+        nc.vector.tensor_copy(first[:], y[:].indirect(pos1_sb[:]))
+        fetch(0)
+        for i in range(len(OUT)):
+            if i + 1 < len(OUT):
+                fetch(i + 1)
+            combine(i)

@@ -1,3 +1,4 @@
+import math
 from contextlib import ExitStack
 
 import concourse.mybir as mybir
@@ -24,10 +25,13 @@ ADD = mybir.AluOpType.add
 IDENT = mybir.ActivationFunctionType.Identity
 
 CHUNK = 512
-GROUPS = [(0, 256), (256, 512), (512, 768), (768, 1024), (1024, 1280), (1280, 1408), (1408, 1536)]
-WIDE = [(0, 512), (512, 1024), (1024, 1536)]
+GROUPS = [(0, 256), (256, 512), (512, 768), (768, 1024), (1024, 1152), (1152, 1280), (1280, 1408), (1408, 1536)]
+THIRDS = [(0, 512), (512, 1024), (1024, 1536)]
+HEAD = [(0, 256), (256, 768), (768, 1536)]
+TAPER = [(0, 768), (768, 1152), (1152, 1408), (1408, 1536)]
 OUT = [(0, 384), (384, 576), (576, 768)]
-TAPER = [(0, 512), (512, 1024), (1024, 1280), (1280, 1408), (1408, 1536)]
+WINDOW = [S + PER_COL, S + PER_COL, T + PER_COL]
+W_EXPERTS = 2
 
 
 def interleave(nc, dst, src):
@@ -42,6 +46,7 @@ def tile_moe_pre_lin_bias_kernel(tc, xT, w, b, gate, offs, pos1, pos2, out):
     with ExitStack() as ctx:
         keep = ctx.enter_context(tc.tile_pool(name="keep", bufs=1))
         ring = ctx.enter_context(tc.tile_pool(name="ring", bufs=4))
+        pair = ctx.enter_context(tc.tile_pool(name="pair", bufs=2))
         psum = ctx.enter_context(tc.psum_pool(name="psum", bufs=1))
 
         offs_sb = keep.tile([P, S // PER_COL], U16, name="offs_sb")
@@ -49,9 +54,8 @@ def tile_moe_pre_lin_bias_kernel(tc, xT, w, b, gate, offs, pos1, pos2, out):
         pos2_sb = keep.tile([P, T // PER_COL], U16, name="pos2_sb")
         b_sb = keep.tile([P, E], F32, name="b_sb")
         gate_sb = keep.tile([P, S], F32, name="gate_sb")
-        win = [[keep.tile([P, T], F32, name=f"win{g}{t}") for t in range(PACK)] for g in range(PASSES)]
+        win = [[keep.tile([P, WINDOW[g]], F32, name=f"win{g}{t}") for t in range(PACK)] for g in range(PASSES)]
         w_raw = [keep.tile([P, E, PACK, N], F32, name=f"w_raw{g}") for g in range(PASSES)]
-        w_bf = [keep.tile([P, E, N, PACK], BF16, name=f"w_bf{g}", align_bytes=64) for g in range(PASSES)]
         w_codes = [keep.tile([P, E * N], U32, name=f"w_codes{g}", align_bytes=64) for g in range(PASSES)]
         w_scales = [keep.tile([P, E * N], U8, name=f"w_scales{g}", align_bytes=64) for g in range(PASSES)]
         x_codes = [keep.tile([P, S], U32, name=f"x_codes{g}", align_bytes=64) for g in range(PASSES)]
@@ -62,50 +66,60 @@ def tile_moe_pre_lin_bias_kernel(tc, xT, w, b, gate, offs, pos1, pos2, out):
         x_rows = xT.rearrange("(g p t) x -> g t p x", g=PASSES, t=PACK)
         w_rows = w.rearrange("e (g p t) n -> g p e t n", g=PASSES, t=PACK)
 
-        def load_gate(lo, hi):
-            nc.sync.dma_start(gate_sb[:, lo:hi], gate[0:P, lo:hi])
+        def load_x(g, planes):
+            for t in planes:
+                nc.sync.dma_start(win[g][t][:, 0:T], x_rows[g, t])
 
+        def load_w(g):
+            for e in range(0, E, W_EXPERTS):
+                nc.sync.dma_start(w_raw[g][:, e : e + W_EXPERTS], w_rows[g][:, e : e + W_EXPERTS])
+
+        load_x(0, [0])
         nc.sync.dma_start(offs_sb[:], offs)
-        nc.sync.dma_start(win[0][0][:], x_rows[0, 0])
-        load_gate(0, 256)
-        load_gate(256, 512)
-        for t in range(1, PACK):
-            nc.sync.dma_start(win[0][t][:], x_rows[0, t])
-        load_gate(*WIDE[1])
-        load_gate(*WIDE[2])
-        for g in range(PASSES):
-            nc.sync.dma_start(w_raw[g][:], w_rows[g])
-            if g + 1 < PASSES:
-                for t in range(PACK):
-                    nc.sync.dma_start(win[g + 1][t][:], x_rows[g + 1, t])
+        for lo, hi in HEAD:
+            nc.sync.dma_start(gate_sb[:, lo:hi], gate[0:P, lo:hi])
+        load_x(0, [1, 2, 3])
+        load_w(0)
+        load_x(1, [0])
+        load_w(1)
+        load_x(1, [1, 2, 3])
+        load_w(2)
+        load_x(2, range(PACK))
         nc.sync.dma_start(b_sb[:], b)
         nc.sync.dma_start(pos1_sb[:], pos1)
         nc.sync.dma_start(pos2_sb[:], pos2)
 
-        def gather(g, lo, hi):
-            picked = ring.tile([P, PACK, CHUNK], F32, name="picked")
-            rounded = ring.tile([P, CHUNK, PACK], BF16, name="rounded", align_bytes=64)
-            n = hi - lo
-            for t in range(PACK):
-                cuts = [lo, 256, hi] if (g, t, lo) == (0, 0, 0) else [lo, hi]
-                for a, z in zip(cuts, cuts[1:]):
-                    nc.vector.tensor_tensor(
-                        picked[:, t, a - lo : z - lo],
-                        win[g][t][:].indirect(offs_sb[:, a // PER_COL : z // PER_COL]),
-                        gate_sb[:, a:z],
-                        MULT,
-                    )
-            interleave(nc, rounded[:, 0:n, :], picked[:, :, 0:n])
-            return rounded
-
-        def quantize_x(g, lo, hi, rounded):
-            nc.vector.quantize_mx(
-                out=x_codes[g][:, lo:hi].bitcast(FP8X4),
-                scales=x_scales[g][:, lo:hi],
-                in_=rounded[:, 0 : hi - lo, :].rearrange("p s t -> p (s t)"),
+        def gather(dst, g, t, lo, hi):
+            nc.vector.tensor_tensor(
+                dst,
+                win[g][t][:].indirect(offs_sb[:, lo // PER_COL : hi // PER_COL]),
+                gate_sb[:, lo:hi],
+                MULT,
             )
 
+        rounded = {}
+
+        def round_x(g, lo, hi, src):
+            tile = ring.tile([P, CHUNK, PACK], BF16, name="x_bf", align_bytes=64)
+            interleave(nc, tile[:, 0 : hi - lo, :], src)
+            rounded[g, lo, hi] = tile
+
+        def quantize_x(g, lo, hi):
+            tile = rounded[g, lo, hi]
+            a = lo
+            while a < hi:
+                z = a + 2 ** int(math.log2(hi - a))
+                nc.vector.quantize_mx(
+                    out=x_codes[g][:, a:z].bitcast(FP8X4),
+                    scales=x_scales[g][:, a:z],
+                    in_=tile[:, a - lo : z - lo, :].rearrange("p s t -> p (s t)"),
+                )
+                a = z
+
+        w_bf = {}
+
         def round_w(g):
+            w_bf[g] = pair.tile([P, E, N, PACK], BF16, name="w_bf", align_bytes=64)
             for e in range(E):
                 interleave(nc, w_bf[g][:, e], w_raw[g][:, e])
 
@@ -130,48 +144,92 @@ def tile_moe_pre_lin_bias_kernel(tc, xT, w, b, gate, offs, pos1, pos2, out):
                         start=(g == 0),
                         stop=(g == PASSES - 1),
                     )
-                    if g == PASSES - 1:
+
+        def empty(lo, hi, on_vector=False):
+            for i, (a, z) in enumerate(GROUPS):
+                if lo <= a and z <= hi:
+                    e = a // C
+                    if on_vector:
+                        nc.vector.tensor_scalar(y[:, a:z], acc[i][:], b_sb[:, e : e + 1], None, ADD)
+                    else:
                         nc.scalar.activation(y[:, a:z], acc[i][:], IDENT, bias=b_sb[:, e : e + 1])
 
-        steps = [(g, lo, hi) for g in range(PASSES) for lo, hi in (TAPER if g == PASSES - 1 else WIDE)]
-        w_round_at = {1: 0, 3: 1, 5: 2}
-        w_quant_at = {2: 0, 4: 1, 6: 2}
-        done_w = set()
-        waiting = []
-        previous = None
-        for i, step in enumerate(steps + [None]):
-            current = None
-            if step is not None:
-                current = (step, gather(*step))
-            if i in w_round_at:
-                round_w(w_round_at[i])
-            if previous is not None:
-                quantize_x(*previous[0], previous[1])
-                waiting.append(previous[0])
-            if i in w_quant_at:
-                quantize_w(w_quant_at[i])
-                done_w.add(w_quant_at[i])
-            for s in list(waiting):
-                if s[0] in done_w:
-                    multiply(*s)
-                    waiting.remove(s)
-            previous = current
+        def finish(g, lo, hi):
+            quantize_x(g, lo, hi)
+            multiply(g, lo, hi)
 
-        first = keep.tile([P, T], F32, name="first")
-        second = [keep.tile([P, hi - lo], F32, name=f"second{lo}") for lo, hi in OUT]
-        total = [keep.tile([P, hi - lo], F32, name=f"total{lo}") for lo, hi in OUT]
+        picked0 = pair.tile([P, PACK, S], F32, name="picked")
+        for lo, hi in HEAD:
+            gather(picked0[:, 0, lo:hi], 0, 0, lo, hi)
+        for t in range(1, PACK):
+            gather(picked0[:, t, :], 0, t, 0, S)
+        round_w(0)
+        round_w(1)
+        for lo, hi in THIRDS:
+            round_x(0, lo, hi, picked0[:, :, lo:hi])
+
+        picked1 = pair.tile([P, PACK, S], F32, name="picked")
+        gather(picked1[:, 0, :], 1, 0, 0, S)
+        quantize_w(0)
+        round_w(2)
+        gather(picked1[:, 1, :], 1, 1, 0, S)
+        finish(0, *THIRDS[0])
+        quantize_w(1)
+        gather(picked1[:, 2, :], 1, 2, 0, S)
+        finish(0, *THIRDS[1])
+        finish(0, *THIRDS[2])
+        gather(picked1[:, 3, 0:CHUNK], 1, 3, 0, CHUNK)
+        gather(picked1[:, 3, CHUNK:S], 1, 3, CHUNK, S)
+        for lo, hi in THIRDS:
+            round_x(1, lo, hi, picked1[:, :, lo:hi])
+        quantize_w(2)
+
+        picked2 = pair.tile([P, PACK * S], F32, name="picked")
+        piece = [picked2[:, PACK * lo : PACK * hi].rearrange("p (t s) -> p t s", t=PACK) for lo, hi in TAPER]
+
+        def gather_last(i, planes):
+            for t in planes:
+                gather(piece[i][:, t, :], 2, t, *TAPER[i])
+
+        gather_last(0, [0, 1])
+        finish(1, *THIRDS[0])
+        gather_last(0, [2, 3])
+        finish(1, *THIRDS[1])
+        round_x(2, 0, 512, piece[0][:, :, 0:512])
+        round_x(2, 512, 768, piece[0][:, :, 512:768])
+        gather_last(1, [0])
+        finish(1, *THIRDS[2])
+        gather_last(1, [1, 2, 3])
+        round_x(2, *TAPER[1], piece[1])
+        finish(2, 0, 512)
+        gather_last(2, [0, 1])
+        finish(2, 512, 768)
+        gather_last(2, [2, 3])
+        round_x(2, *TAPER[2], piece[2])
+        empty(0, 768)
+        gather_last(3, range(PACK))
+        round_x(2, *TAPER[3], piece[3])
+        finish(2, *TAPER[1])
+        finish(2, *TAPER[2])
+        finish(2, *TAPER[3])
+        empty(*TAPER[1])
+        empty(*TAPER[2], on_vector=True)
+        empty(*TAPER[3])
+
+        ends = pair.tile([P, 3, T], F32, name="picked")
+        first, second, total = ends[:, 0, :], ends[:, 1, :], ends[:, 2, :]
 
         def fetch(i):
             lo, hi = OUT[i]
-            nc.vector.tensor_copy(second[i][:], y[:].indirect(pos2_sb[:, lo // PER_COL : hi // PER_COL]))
+            nc.vector.tensor_copy(second[:, lo:hi], y[:].indirect(pos2_sb[:, lo // PER_COL : hi // PER_COL]))
 
         def combine(i):
             lo, hi = OUT[i]
-            nc.vector.tensor_tensor(total[i][:], first[:, lo:hi], second[i][:], ADD)
+            nc.vector.tensor_tensor(total[:, lo:hi], first[:, lo:hi], second[:, lo:hi], ADD)
             queue = nc.scalar if i % 2 else nc.sync
-            queue.dma_start(out[:, lo:hi], total[i][:])
+            queue.dma_start(out[:, lo:hi], total[:, lo:hi])
 
-        nc.vector.tensor_copy(first[:], y[:].indirect(pos1_sb[:]))
+        nc.vector.tensor_copy(first, y[:].indirect(pos1_sb[:]))
         fetch(0)
         for i in range(len(OUT)):
             if i + 1 < len(OUT):

@@ -1,4 +1,3 @@
-import math
 from contextlib import ExitStack
 
 import concourse.mybir as mybir
@@ -24,13 +23,10 @@ MULT = mybir.AluOpType.mult
 ADD = mybir.AluOpType.add
 IDENT = mybir.ActivationFunctionType.Identity
 
-CHUNK = 512
-GROUPS = [(0, 256), (256, 512), (512, 768), (768, 1024), (1024, 1152), (1152, 1280), (1280, 1408), (1408, 1536)]
-THIRDS = [(0, 512), (512, 1024), (1024, 1536)]
 HEAD = [(0, 256), (256, 768), (768, 1536)]
-TAPER = [(0, 768), (768, 1152), (1152, 1408), (1408, 1536)]
+GROUPS = [(0, 256), (256, 512), (512, 768), (768, 1024), (1024, 1280), (1280, 1408), (1408, 1536)]
 OUT = [(0, 384), (384, 576), (576, 768)]
-WINDOW = [S + PER_COL, S + PER_COL, T + PER_COL]
+WINDOW = S + PER_COL
 W_EXPERTS = 2
 
 
@@ -45,7 +41,8 @@ def tile_moe_pre_lin_bias_kernel(tc, xT, w, b, gate, offs, pos1, pos2, out):
     nc = tc.nc
     with ExitStack() as ctx:
         keep = ctx.enter_context(tc.tile_pool(name="keep", bufs=1))
-        ring = ctx.enter_context(tc.tile_pool(name="ring", bufs=4))
+        windows = ctx.enter_context(tc.tile_pool(name="windows", bufs=2 * PACK))
+        stage = ctx.enter_context(tc.tile_pool(name="stage", bufs=PASSES))
         pair = ctx.enter_context(tc.tile_pool(name="pair", bufs=2))
         psum = ctx.enter_context(tc.psum_pool(name="psum", bufs=1))
 
@@ -54,10 +51,9 @@ def tile_moe_pre_lin_bias_kernel(tc, xT, w, b, gate, offs, pos1, pos2, out):
         pos2_sb = keep.tile([P, T // PER_COL], U16, name="pos2_sb")
         b_sb = keep.tile([P, E], F32, name="b_sb")
         gate_sb = keep.tile([P, S], F32, name="gate_sb")
-        win = [[keep.tile([P, WINDOW[g]], F32, name=f"win{g}{t}") for t in range(PACK)] for g in range(PASSES)]
-        w_raw = [keep.tile([P, E, PACK, N], F32, name=f"w_raw{g}") for g in range(PASSES)]
-        w_codes = [keep.tile([P, E * N], U32, name=f"w_codes{g}", align_bytes=64) for g in range(PASSES)]
-        w_scales = [keep.tile([P, E * N], U8, name=f"w_scales{g}", align_bytes=64) for g in range(PASSES)]
+        w_bf = keep.tile([P, PASSES * E, N, PACK], BF16, name="w_bf", align_bytes=64)
+        w_codes = keep.tile([P, PASSES * E * N], U32, name="w_codes", align_bytes=64)
+        w_scales = keep.tile([P, PASSES * E * N], U8, name="w_scales", align_bytes=64)
         x_codes = [keep.tile([P, S], U32, name=f"x_codes{g}", align_bytes=64) for g in range(PASSES)]
         x_scales = [keep.tile([P, S], U8, name=f"x_scales{g}", align_bytes=64) for g in range(PASSES)]
         y = keep.tile([P, S], F32, name="y")
@@ -65,12 +61,16 @@ def tile_moe_pre_lin_bias_kernel(tc, xT, w, b, gate, offs, pos1, pos2, out):
 
         x_rows = xT.rearrange("(g p t) x -> g t p x", g=PASSES, t=PACK)
         w_rows = w.rearrange("e (g p t) n -> g p e t n", g=PASSES, t=PACK)
+        win = {}
+        w_raw = {}
 
         def load_x(g, planes):
             for t in planes:
-                nc.sync.dma_start(win[g][t][:, 0:T], x_rows[g, t])
+                win[g, t] = windows.tile([P, WINDOW], F32, name="win")
+                nc.sync.dma_start(win[g, t][:, 0:T], x_rows[g, t])
 
         def load_w(g):
+            w_raw[g] = stage.tile([P, E, PACK, N], F32, name="stage", align_bytes=64)
             for e in range(0, E, W_EXPERTS):
                 nc.sync.dma_start(w_raw[g][:, e : e + W_EXPERTS], w_rows[g][:, e : e + W_EXPERTS])
 
@@ -84,137 +84,117 @@ def tile_moe_pre_lin_bias_kernel(tc, xT, w, b, gate, offs, pos1, pos2, out):
         load_w(1)
         load_x(1, [1, 2, 3])
         load_w(2)
-        load_x(2, range(PACK))
         nc.sync.dma_start(b_sb[:], b)
         nc.sync.dma_start(pos1_sb[:], pos1)
         nc.sync.dma_start(pos2_sb[:], pos2)
 
-        def gather(dst, g, t, lo, hi):
-            nc.vector.tensor_tensor(
-                dst,
-                win[g][t][:].indirect(offs_sb[:, lo // PER_COL : hi // PER_COL]),
-                gate_sb[:, lo:hi],
-                MULT,
-            )
+        picked = {}
+        x_bf = {}
 
-        rounded = {}
-
-        def round_x(g, lo, hi, src):
-            tile = ring.tile([P, CHUNK, PACK], BF16, name="x_bf", align_bytes=64)
-            interleave(nc, tile[:, 0 : hi - lo, :], src)
-            rounded[g, lo, hi] = tile
-
-        def quantize_x(g, lo, hi):
-            tile = rounded[g, lo, hi]
-            a = lo
-            while a < hi:
-                z = a + 2 ** int(math.log2(hi - a))
-                nc.vector.quantize_mx(
-                    out=x_codes[g][:, a:z].bitcast(FP8X4),
-                    scales=x_scales[g][:, a:z],
-                    in_=tile[:, a - lo : z - lo, :].rearrange("p s t -> p (s t)"),
+        def gather(g, t, pieces):
+            if t == 0:
+                picked[g] = pair.tile([P, PACK, S], F32, name="picked")
+            for lo, hi in pieces:
+                nc.vector.tensor_tensor(
+                    picked[g][:, t, lo:hi],
+                    win[g, t][:].indirect(offs_sb[:, lo // PER_COL : hi // PER_COL]),
+                    gate_sb[:, lo:hi],
+                    MULT,
                 )
-                a = z
 
-        w_bf = {}
+        def round_x(g, pieces):
+            x_bf[g] = stage.tile([P, S, PACK], BF16, name="stage", align_bytes=64)
+            for lo, hi in pieces:
+                interleave(nc, x_bf[g][:, lo:hi, :], picked[g][:, :, lo:hi])
 
         def round_w(g):
-            w_bf[g] = pair.tile([P, E, N, PACK], BF16, name="w_bf", align_bytes=64)
             for e in range(E):
-                interleave(nc, w_bf[g][:, e], w_raw[g][:, e])
+                interleave(nc, w_bf[:, g * E + e], w_raw[g][:, e])
 
-        def quantize_w(g):
-            for e0, e1 in ((0, 4), (4, 6)):
-                nc.vector.quantize_mx(
-                    out=w_codes[g][:, e0 * N : e1 * N].bitcast(FP8X4),
-                    scales=w_scales[g][:, e0 * N : e1 * N],
-                    in_=w_bf[g][:, e0:e1].rearrange("p e n t -> p (e n t)"),
-                )
+        w_done = set()
+        x_done = set()
+        passes_done = [0] * len(GROUPS)
+        multiplied = set()
 
-        def multiply(g, lo, hi):
-            for i, (a, z) in enumerate(GROUPS):
-                if lo <= a and z <= hi:
-                    e = a // C
+        def multiply_ready():
+            for g in range(PASSES):
+                for i, (lo, hi) in enumerate(GROUPS):
+                    m = g * E + lo // C
+                    if (g, i) in multiplied or m not in w_done or (g, i) not in x_done:
+                        continue
                     nc.tensor.matmul_mx(
                         out=acc[i][:],
-                        lhsT=w_codes[g][:, e * N : (e + 1) * N].bitcast(FP8X4),
-                        lhsT_scale=w_scales[g][:, e * N : (e + 1) * N],
-                        rhs=x_codes[g][:, a:z].bitcast(FP8X4),
-                        rhs_scale=x_scales[g][:, a:z],
-                        start=(g == 0),
-                        stop=(g == PASSES - 1),
+                        lhsT=w_codes[:, m * N : (m + 1) * N].bitcast(FP8X4),
+                        lhsT_scale=w_scales[:, m * N : (m + 1) * N],
+                        rhs=x_codes[g][:, lo:hi].bitcast(FP8X4),
+                        rhs_scale=x_scales[g][:, lo:hi],
+                        start=(passes_done[i] == 0),
+                        stop=(passes_done[i] == PASSES - 1),
                     )
+                    passes_done[i] += 1
+                    multiplied.add((g, i))
 
-        def empty(lo, hi, on_vector=False):
+        def quantize_x(g, lo, hi):
+            nc.vector.quantize_mx(
+                out=x_codes[g][:, lo:hi].bitcast(FP8X4),
+                scales=x_scales[g][:, lo:hi],
+                in_=x_bf[g][:, lo:hi, :].rearrange("p s t -> p (s t)"),
+            )
             for i, (a, z) in enumerate(GROUPS):
                 if lo <= a and z <= hi:
-                    e = a // C
-                    if on_vector:
-                        nc.vector.tensor_scalar(y[:, a:z], acc[i][:], b_sb[:, e : e + 1], None, ADD)
-                    else:
-                        nc.scalar.activation(y[:, a:z], acc[i][:], IDENT, bias=b_sb[:, e : e + 1])
+                    x_done.add((g, i))
+            multiply_ready()
 
-        def finish(g, lo, hi):
-            quantize_x(g, lo, hi)
-            multiply(g, lo, hi)
+        def quantize_w(m0, m1):
+            nc.vector.quantize_mx(
+                out=w_codes[:, m0 * N : m1 * N].bitcast(FP8X4),
+                scales=w_scales[:, m0 * N : m1 * N],
+                in_=w_bf[:, m0:m1].rearrange("p m n t -> p (m n t)"),
+            )
+            for m in range(m0, m1):
+                w_done.add(m)
+            multiply_ready()
 
-        picked0 = pair.tile([P, PACK, S], F32, name="picked")
-        for lo, hi in HEAD:
-            gather(picked0[:, 0, lo:hi], 0, 0, lo, hi)
+        def empty(i, on_vector=False):
+            lo, hi = GROUPS[i]
+            e = lo // C
+            if on_vector:
+                nc.vector.tensor_scalar(y[:, lo:hi], acc[i][:], b_sb[:, e : e + 1], None, ADD)
+            else:
+                nc.scalar.activation(y[:, lo:hi], acc[i][:], IDENT, bias=b_sb[:, e : e + 1])
+
+        whole = [(0, S)]
+        gather(0, 0, HEAD)
         for t in range(1, PACK):
-            gather(picked0[:, t, :], 0, t, 0, S)
+            gather(0, t, whole)
+        load_x(2, range(PACK))
         round_w(0)
         round_w(1)
-        for lo, hi in THIRDS:
-            round_x(0, lo, hi, picked0[:, :, lo:hi])
-
-        picked1 = pair.tile([P, PACK, S], F32, name="picked")
-        gather(picked1[:, 0, :], 1, 0, 0, S)
-        quantize_w(0)
+        round_x(0, [(0, 1024), (1024, 1536)])
         round_w(2)
-        gather(picked1[:, 1, :], 1, 1, 0, S)
-        finish(0, *THIRDS[0])
-        quantize_w(1)
-        gather(picked1[:, 2, :], 1, 2, 0, S)
-        finish(0, *THIRDS[1])
-        finish(0, *THIRDS[2])
-        gather(picked1[:, 3, 0:CHUNK], 1, 3, 0, CHUNK)
-        gather(picked1[:, 3, CHUNK:S], 1, 3, CHUNK, S)
-        for lo, hi in THIRDS:
-            round_x(1, lo, hi, picked1[:, :, lo:hi])
-        quantize_w(2)
-
-        picked2 = pair.tile([P, PACK * S], F32, name="picked")
-        piece = [picked2[:, PACK * lo : PACK * hi].rearrange("p (t s) -> p t s", t=PACK) for lo, hi in TAPER]
-
-        def gather_last(i, planes):
-            for t in planes:
-                gather(piece[i][:, t, :], 2, t, *TAPER[i])
-
-        gather_last(0, [0, 1])
-        finish(1, *THIRDS[0])
-        gather_last(0, [2, 3])
-        finish(1, *THIRDS[1])
-        round_x(2, 0, 512, piece[0][:, :, 0:512])
-        round_x(2, 512, 768, piece[0][:, :, 512:768])
-        gather_last(1, [0])
-        finish(1, *THIRDS[2])
-        gather_last(1, [1, 2, 3])
-        round_x(2, *TAPER[1], piece[1])
-        finish(2, 0, 512)
-        gather_last(2, [0, 1])
-        finish(2, 512, 768)
-        gather_last(2, [2, 3])
-        round_x(2, *TAPER[2], piece[2])
-        empty(0, 768)
-        gather_last(3, range(PACK))
-        round_x(2, *TAPER[3], piece[3])
-        finish(2, *TAPER[1])
-        finish(2, *TAPER[2])
-        finish(2, *TAPER[3])
-        empty(*TAPER[1])
-        empty(*TAPER[2], on_vector=True)
-        empty(*TAPER[3])
+        gather(1, 0, whole)
+        gather(1, 1, whole)
+        quantize_w(0, 8)
+        gather(1, 2, whole)
+        gather(1, 3, whole)
+        quantize_x(0, 0, 1024)
+        round_x(1, [(0, 1024), (1024, 1536)])
+        for t in range(PACK - 1):
+            gather(2, t, whole)
+        gather(2, PACK - 1, HEAD)
+        round_x(2, [(0, 256), (256, 768), (768, 1024), (1024, 1280), (1280, 1536)])
+        quantize_x(1, 0, 1024)
+        quantize_w(8, 16)
+        quantize_x(0, 1024, 1536)
+        quantize_x(1, 1024, 1536)
+        quantize_x(2, 0, 512)
+        quantize_x(2, 512, 1024)
+        quantize_w(16, 18)
+        quantize_x(2, 1024, 1280)
+        quantize_x(2, 1280, 1408)
+        quantize_x(2, 1408, 1536)
+        for i in range(len(GROUPS)):
+            empty(i, on_vector=(i in (4, 6)))
 
         ends = pair.tile([P, 3, T], F32, name="picked")
         first, second, total = ends[:, 0, :], ends[:, 1, :], ends[:, 2, :]

@@ -199,19 +199,18 @@ def tile_moe_pre_lin_bias_kernel(tc, xT, w, b, gate, offs, pos1, pos2, out):
         ends = pair.tile([P, 3, T], F32, name="picked")
         first, second, total = ends[:, 0, :], ends[:, 1, :], ends[:, 2, :]
 
-        def fetch(i):
-            lo, hi = OUT[i]
-            nc.vector.tensor_copy(second[:, lo:hi], y[:].indirect(pos2_sb[:, lo // PER_COL : hi // PER_COL]))
+        def fetch(dst, positions, lo, hi):
+            nc.vector.tensor_copy(dst[:, lo:hi], y[:].indirect(positions[:, lo // PER_COL : hi // PER_COL]))
 
-        def combine(i):
-            lo, hi = OUT[i]
-            nc.vector.tensor_tensor(total[:, lo:hi], first[:, lo:hi], second[:, lo:hi], ADD)
-            queue = nc.scalar if i % 2 else nc.sync
+        def combine(engine, queue, lo, hi):
+            engine.tensor_tensor(total[:, lo:hi], first[:, lo:hi], second[:, lo:hi], ADD)
             queue.dma_start(out[:, lo:hi], total[:, lo:hi])
 
-        nc.vector.tensor_copy(first, y[:].indirect(pos1_sb[:]))
-        fetch(0)
-        for i in range(len(OUT)):
-            if i + 1 < len(OUT):
-                fetch(i + 1)
-            combine(i)
+        fetch(first, pos1_sb, *OUT[0])
+        fetch(second, pos2_sb, *OUT[0])
+        combine(nc.gpsimd, nc.sync, *OUT[0])
+        fetch(first, pos1_sb, OUT[1][0], T)
+        fetch(second, pos2_sb, *OUT[1])
+        fetch(second, pos2_sb, *OUT[2])
+        combine(nc.vector, nc.scalar, *OUT[1])
+        combine(nc.vector, nc.sync, *OUT[2])

@@ -25,7 +25,8 @@ IDENT = mybir.ActivationFunctionType.Identity
 
 HEAD = [(0, 256), (256, 768), (768, 1536)]
 GROUPS = [(0, 256), (256, 512), (512, 768), (768, 1024), (1024, 1280), (1280, 1408), (1408, 1536)]
-OUT = [(0, 384), (384, 576), (576, 768)]
+FETCH = [(0, 384), (384, 768)]
+OUT = [(0, 384), (384, 640), (640, 768)]
 WINDOW = S + PER_COL
 W_EXPERTS = 2
 
@@ -196,21 +197,13 @@ def tile_moe_pre_lin_bias_kernel(tc, xT, w, b, gate, offs, pos1, pos2, out):
         for i in range(len(GROUPS)):
             empty(i, on_vector=(i in (4, 6)))
 
-        ends = pair.tile([P, 3, T], F32, name="picked")
-        first, second, total = ends[:, 0, :], ends[:, 1, :], ends[:, 2, :]
+        ends = pair.tile([P, 2, T], F32, name="picked")
+        first, total = ends[:, 0, :], ends[:, 1, :]
 
-        def fetch(dst, positions, lo, hi):
-            nc.vector.tensor_copy(dst[:, lo:hi], y[:].indirect(positions[:, lo // PER_COL : hi // PER_COL]))
-
-        def combine(engine, queue, lo, hi):
-            engine.tensor_tensor(total[:, lo:hi], first[:, lo:hi], second[:, lo:hi], ADD)
-            queue.dma_start(out[:, lo:hi], total[:, lo:hi])
-
-        fetch(first, pos1_sb, *OUT[0])
-        fetch(second, pos2_sb, *OUT[0])
-        combine(nc.gpsimd, nc.sync, *OUT[0])
-        fetch(first, pos1_sb, OUT[1][0], T)
-        fetch(second, pos2_sb, *OUT[1])
-        fetch(second, pos2_sb, *OUT[2])
-        combine(nc.vector, nc.scalar, *OUT[1])
-        combine(nc.vector, nc.sync, *OUT[2])
+        for lo, hi in FETCH:
+            nc.vector.tensor_copy(first[:, lo:hi], y[:].indirect(pos1_sb[:, lo // PER_COL : hi // PER_COL]))
+        for i, (lo, hi) in enumerate(OUT):
+            nc.vector.tensor_tensor(
+                total[:, lo:hi], y[:].indirect(pos2_sb[:, lo // PER_COL : hi // PER_COL]), first[:, lo:hi], ADD
+            )
+            (nc.sync if i % 2 == 0 else nc.scalar).dma_start(out[:, lo:hi], total[:, lo:hi])

@@ -23,7 +23,8 @@ MULT = mybir.AluOpType.mult
 ADD = mybir.AluOpType.add
 IDENT = mybir.ActivationFunctionType.Identity
 
-HEAD = [(0, 256), (256, 768), (768, 1536)]
+HEAD = [(0, 128), (128, 448), (448, 1024), (1024, 1536)]
+LAST = [(0, 256), (256, 768), (768, 1536)]
 GROUPS = [(0, 256), (256, 512), (512, 768), (768, 1024), (1024, 1280), (1280, 1408), (1408, 1536)]
 FETCH = [(0, 384), (384, 768)]
 OUT = [(0, 384), (384, 640), (640, 768)]
@@ -182,7 +183,7 @@ def tile_moe_pre_lin_bias_kernel(tc, xT, w, b, gate, offs, pos1, pos2, out):
         round_x(1, [(0, 1024), (1024, 1536)])
         for t in range(PACK - 1):
             gather(2, t, whole)
-        gather(2, PACK - 1, HEAD)
+        gather(2, PACK - 1, LAST)
         round_x(2, [(0, 256), (256, 768), (768, 1024), (1024, 1280), (1280, 1536)])
         quantize_x(1, 0, 1024)
         quantize_w(8, 16)
@@ -195,7 +196,7 @@ def tile_moe_pre_lin_bias_kernel(tc, xT, w, b, gate, offs, pos1, pos2, out):
         quantize_x(2, 1280, 1408)
         quantize_x(2, 1408, 1536)
         for i in range(len(GROUPS)):
-            empty(i, on_vector=(i in (4, 6)))
+            empty(i, on_vector=(i == 5))
 
         ends = pair.tile([P, 2, T], F32, name="picked")
         first, total = ends[:, 0, :], ends[:, 1, :]

@@ -31,6 +31,19 @@ OUT = [(0, 384), (384, 640), (640, 768)]
 WINDOW = S + PER_COL
 W_EXPERTS = 2
 
+BATCHES = [
+    [("w", 0, 0, 6), ("w", 1, 0, 2)],
+    [("x", 0, 0, 1024)],
+    [("w", 1, 2, 5), ("w", 2, 0, 5)],
+    [("x", 1, 0, 1024)],
+    [("x", 2, 0, 256), ("x", 0, 1024, 1536), ("x", 1, 1024, 1280)],
+    [("x", 2, 256, 768)],
+    [("x", 2, 768, 1280)],
+    [("w", 1, 5, 6), ("w", 2, 5, 6), ("x", 1, 1280, 1536)],
+    [("x", 2, 1280, 1536)],
+]
+HELD = 7
+
 
 def interleave(nc, dst, src):
     nc.scalar.copy(
@@ -39,13 +52,17 @@ def interleave(nc, dst, src):
     )
 
 
+def width(run):
+    kind, g, lo, hi = run
+    return (hi - lo) * (N if kind == "w" else 1)
+
+
 def tile_moe_pre_lin_bias_kernel(tc, xT, w, b, gate, offs, pos1, pos2, out):
     nc = tc.nc
     with ExitStack() as ctx:
         keep = ctx.enter_context(tc.tile_pool(name="keep", bufs=1))
         windows = ctx.enter_context(tc.tile_pool(name="windows", bufs=2 * PACK))
-        stage = ctx.enter_context(tc.tile_pool(name="stage", bufs=PASSES))
-        pair = ctx.enter_context(tc.tile_pool(name="pair", bufs=2))
+        turns = ctx.enter_context(tc.tile_pool(name="turns", bufs=1))
         psum = ctx.enter_context(tc.psum_pool(name="psum", bufs=1))
 
         offs_sb = keep.tile([P, S // PER_COL], U16, name="offs_sb")
@@ -53,13 +70,17 @@ def tile_moe_pre_lin_bias_kernel(tc, xT, w, b, gate, offs, pos1, pos2, out):
         pos2_sb = keep.tile([P, T // PER_COL], U16, name="pos2_sb")
         b_sb = keep.tile([P, E], F32, name="b_sb")
         gate_sb = keep.tile([P, S], F32, name="gate_sb")
-        w_bf = keep.tile([P, PASSES * E, N, PACK], BF16, name="w_bf", align_bytes=64)
-        w_codes = keep.tile([P, PASSES * E * N], U32, name="w_codes", align_bytes=64)
-        w_scales = keep.tile([P, PASSES * E * N], U8, name="w_scales", align_bytes=64)
-        x_codes = [keep.tile([P, S], U32, name=f"x_codes{g}", align_bytes=64) for g in range(PASSES)]
-        x_scales = [keep.tile([P, S], U8, name=f"x_scales{g}", align_bytes=64) for g in range(PASSES)]
         y = keep.tile([P, S], F32, name="y")
         acc = [psum.tile([P, hi - lo], F32, name=f"acc{i}") for i, (lo, hi) in enumerate(GROUPS)]
+
+        widths = [sum(width(run) for run in batch) for batch in BATCHES]
+        rounded = [keep.tile([P, n, PACK], BF16, name=f"rounded{q}", align_bytes=64) for q, n in enumerate(widths)]
+        scales = [keep.tile([P, n], U8, name=f"scales{q}", align_bytes=64) for q, n in enumerate(widths)]
+        codes = {}
+        start = {}
+        for q, batch in enumerate(BATCHES):
+            for j, run in enumerate(batch):
+                start[run] = (q, sum(width(r) for r in batch[:j]))
 
         x_rows = xT.rearrange("(g p t) x -> g t p x", g=PASSES, t=PACK)
         w_rows = w.rearrange("e (g p t) n -> g p e t n", g=PASSES, t=PACK)
@@ -72,7 +93,7 @@ def tile_moe_pre_lin_bias_kernel(tc, xT, w, b, gate, offs, pos1, pos2, out):
                 nc.sync.dma_start(win[g, t][:, 0:T], x_rows[g, t])
 
         def load_w(g):
-            w_raw[g] = stage.tile([P, E, PACK, N], F32, name="stage", align_bytes=64)
+            w_raw[g] = keep.tile([P, E, PACK, N], F32, name=f"w_raw{g}")
             for e in range(0, E, W_EXPERTS):
                 nc.sync.dma_start(w_raw[g][:, e : e + W_EXPERTS], w_rows[g][:, e : e + W_EXPERTS])
 
@@ -91,11 +112,10 @@ def tile_moe_pre_lin_bias_kernel(tc, xT, w, b, gate, offs, pos1, pos2, out):
         nc.sync.dma_start(pos2_sb[:], pos2)
 
         picked = {}
-        x_bf = {}
 
         def gather(g, t, pieces):
             if t == 0:
-                picked[g] = pair.tile([P, PACK, S], F32, name="picked")
+                picked[g] = turns.tile([P, PACK, S], F32, name=f"turn{g % 2}", align_bytes=64)
             for lo, hi in pieces:
                 nc.vector.tensor_tensor(
                     picked[g][:, t, lo:hi],
@@ -104,60 +124,66 @@ def tile_moe_pre_lin_bias_kernel(tc, xT, w, b, gate, offs, pos1, pos2, out):
                     MULT,
                 )
 
-        def round_x(g, pieces):
-            x_bf[g] = stage.tile([P, S, PACK], BF16, name="stage", align_bytes=64)
-            for lo, hi in pieces:
-                interleave(nc, x_bf[g][:, lo:hi, :], picked[g][:, :, lo:hi])
+        def runs_of(kind, g):
+            return sorted(run for run in start if run[:2] == (kind, g))
+
+        def round_x(g):
+            for run in runs_of("x", g):
+                q, at = start[run]
+                interleave(nc, rounded[q][:, at : at + width(run), :], picked[g][:, :, run[2] : run[3]])
 
         def round_w(g):
-            for e in range(E):
-                interleave(nc, w_bf[:, g * E + e], w_raw[g][:, e])
+            for run in runs_of("w", g):
+                q, at = start[run]
+                for e in range(run[2], run[3]):
+                    first = at + (e - run[2]) * N
+                    interleave(nc, rounded[q][:, first : first + N, :], w_raw[g][:, e])
 
-        w_done = set()
-        x_done = set()
+        def columns(kind, g, lo, n):
+            run = [r for r in runs_of(kind, g) if r[2] <= lo < r[3]][0]
+            q, at = start[run]
+            first = at + (lo - run[2]) * (N if kind == "w" else 1)
+            return q, slice(first, first + n)
+
         passes_done = [0] * len(GROUPS)
         multiplied = set()
+        done = [0] * len(BATCHES)
 
         def multiply_ready():
-            for g in range(PASSES):
-                for i, (lo, hi) in enumerate(GROUPS):
-                    m = g * E + lo // C
-                    if (g, i) in multiplied or m not in w_done or (g, i) not in x_done:
+            for i, (lo, hi) in enumerate(GROUPS):
+                for g in range(PASSES):
+                    qw, w_cols = columns("w", g, lo // C, N)
+                    qx, x_cols = columns("x", g, lo, hi - lo)
+                    if (g, i) in multiplied or done[qw] < w_cols.stop or done[qx] < x_cols.stop:
                         continue
                     nc.tensor.matmul_mx(
                         out=acc[i][:],
-                        lhsT=w_codes[:, m * N : (m + 1) * N].bitcast(FP8X4),
-                        lhsT_scale=w_scales[:, m * N : (m + 1) * N],
-                        rhs=x_codes[g][:, lo:hi].bitcast(FP8X4),
-                        rhs_scale=x_scales[g][:, lo:hi],
+                        lhsT=codes[qw][:, w_cols].bitcast(FP8X4),
+                        lhsT_scale=scales[qw][:, w_cols],
+                        rhs=codes[qx][:, x_cols].bitcast(FP8X4),
+                        rhs_scale=scales[qx][:, x_cols],
                         start=(passes_done[i] == 0),
                         stop=(passes_done[i] == PASSES - 1),
                     )
                     passes_done[i] += 1
                     multiplied.add((g, i))
 
-        def quantize_x(g, lo, hi):
-            nc.vector.quantize_mx(
-                out=x_codes[g][:, lo:hi].bitcast(FP8X4),
-                scales=x_scales[g][:, lo:hi],
-                in_=x_bf[g][:, lo:hi, :].rearrange("p s t -> p (s t)"),
-            )
-            for i, (a, z) in enumerate(GROUPS):
-                if lo <= a and z <= hi:
-                    x_done.add((g, i))
-            multiply_ready()
+        def quantize(q, calls=1):
+            if q == HELD:
+                codes[q] = turns.tile([P, widths[q]], U32, name="turn0", align_bytes=64)
+            else:
+                codes[q] = keep.tile([P, widths[q]], U32, name=f"codes{q}", align_bytes=64)
+            for c in range(calls):
+                cols = slice(c * widths[q] // calls, (c + 1) * widths[q] // calls)
+                nc.vector.quantize_mx(
+                    out=codes[q][:, cols].bitcast(FP8X4),
+                    scales=scales[q][:, cols],
+                    in_=rounded[q][:, cols, :].rearrange("p s t -> p (s t)"),
+                )
+                done[q] = cols.stop
+                multiply_ready()
 
-        def quantize_w(m0, m1):
-            nc.vector.quantize_mx(
-                out=w_codes[:, m0 * N : m1 * N].bitcast(FP8X4),
-                scales=w_scales[:, m0 * N : m1 * N],
-                in_=w_bf[:, m0:m1].rearrange("p m n t -> p (m n t)"),
-            )
-            for m in range(m0, m1):
-                w_done.add(m)
-            multiply_ready()
-
-        def empty(i, on_vector=False):
+        def empty(i, on_vector):
             lo, hi = GROUPS[i]
             e = lo // C
             if on_vector:
@@ -172,33 +198,26 @@ def tile_moe_pre_lin_bias_kernel(tc, xT, w, b, gate, offs, pos1, pos2, out):
         load_x(2, range(PACK))
         round_w(0)
         round_w(1)
-        round_x(0, [(0, 1024), (1024, 1536)])
+        round_x(0)
         round_w(2)
         gather(1, 0, whole)
         gather(1, 1, whole)
-        quantize_w(0, 8)
+        quantize(0)
         gather(1, 2, whole)
         gather(1, 3, whole)
-        quantize_x(0, 0, 1024)
-        round_x(1, [(0, 1024), (1024, 1536)])
+        quantize(1)
+        round_x(1)
         for t in range(PACK - 1):
             gather(2, t, whole)
         gather(2, PACK - 1, LAST)
-        round_x(2, [(0, 256), (256, 768), (768, 1024), (1024, 1280), (1280, 1536)])
-        quantize_x(1, 0, 1024)
-        quantize_w(8, 16)
-        quantize_x(0, 1024, 1536)
-        quantize_x(1, 1024, 1536)
-        quantize_x(2, 0, 512)
-        quantize_x(2, 512, 1024)
-        quantize_w(16, 18)
-        quantize_x(2, 1024, 1280)
-        quantize_x(2, 1280, 1408)
-        quantize_x(2, 1408, 1536)
+        round_x(2)
+        for q in range(2, len(BATCHES) - 1):
+            quantize(q)
+        quantize(len(BATCHES) - 1, calls=2)
         for i in range(len(GROUPS)):
-            empty(i, on_vector=(i == 5))
+            empty(i, on_vector=(i >= 5))
 
-        ends = pair.tile([P, 2, T], F32, name="picked")
+        ends = turns.tile([P, 2, T], F32, name="turn1", align_bytes=64)
         first, total = ends[:, 0, :], ends[:, 1, :]
 
         for lo, hi in FETCH:

@@ -24,7 +24,7 @@ ADD = mybir.AluOpType.add
 IDENT = mybir.ActivationFunctionType.Identity
 
 HEAD = [(0, 128), (128, 448), (448, 1024), (1024, 1536)]
-LAST = [(0, 256), (256, 768), (768, 1536)]
+LAST = [(0, 768), (768, 1536)]
 GROUPS = [(0, 256), (256, 512), (512, 768), (768, 1024), (1024, 1280), (1280, 1408), (1408, 1536)]
 FETCH = [(0, 384), (384, 768)]
 OUT = [(0, 384), (384, 640), (640, 768)]
@@ -34,15 +34,14 @@ W_EXPERTS = 2
 BATCHES = [
     [("w", 0, 0, 6), ("w", 1, 0, 2)],
     [("x", 0, 0, 1024)],
-    [("w", 1, 2, 5), ("w", 2, 0, 5)],
+    [("w", 1, 2, 6), ("w", 2, 0, 4)],
     [("x", 1, 0, 1024)],
-    [("x", 2, 0, 256), ("x", 0, 1024, 1536), ("x", 1, 1024, 1280)],
-    [("x", 2, 256, 768)],
-    [("x", 2, 768, 1280)],
-    [("w", 1, 5, 6), ("w", 2, 5, 6), ("x", 1, 1280, 1536)],
+    [("x", 2, 0, 768), ("w", 2, 4, 6)],
+    [("x", 2, 768, 1280), ("x", 0, 1024, 1280), ("x", 1, 1024, 1280)],
+    [("x", 0, 1280, 1536), ("x", 1, 1280, 1536)],
     [("x", 2, 1280, 1536)],
 ]
-HELD = 7
+HELD = 6
 
 
 def interleave(nc, dst, src):
@@ -75,7 +74,7 @@ def tile_moe_pre_lin_bias_kernel(tc, xT, w, b, gate, offs, pos1, pos2, out):
 
         widths = [sum(width(run) for run in batch) for batch in BATCHES]
         rounded = [keep.tile([P, n, PACK], BF16, name=f"rounded{q}", align_bytes=64) for q, n in enumerate(widths)]
-        scales = [keep.tile([P, n], U8, name=f"scales{q}", align_bytes=64) for q, n in enumerate(widths)]
+        scales = {0: keep.tile([P, widths[0]], U8, name="scales0", align_bytes=64)}
         codes = {}
         start = {}
         for q, batch in enumerate(BATCHES):
@@ -89,7 +88,10 @@ def tile_moe_pre_lin_bias_kernel(tc, xT, w, b, gate, offs, pos1, pos2, out):
 
         def load_x(g, planes):
             for t in planes:
-                win[g, t] = windows.tile([P, WINDOW], F32, name="win")
+                if (g, t) == (PASSES - 1, PACK - 2):
+                    win[g, t] = turns.tile([P, WINDOW], F32, name="last", align_bytes=64)
+                else:
+                    win[g, t] = windows.tile([P, WINDOW], F32, name="win")
                 nc.sync.dma_start(win[g, t][:, 0:T], x_rows[g, t])
 
         def load_w(g):
@@ -205,17 +207,19 @@ def tile_moe_pre_lin_bias_kernel(tc, xT, w, b, gate, offs, pos1, pos2, out):
         quantize(0)
         gather(1, 2, whole)
         gather(1, 3, whole)
-        quantize(1)
         round_x(1)
         for t in range(PACK - 1):
             gather(2, t, whole)
         gather(2, PACK - 1, LAST)
         round_x(2)
-        for q in range(2, len(BATCHES) - 1):
+        late = turns.tile([P, sum(widths[1:])], U8, name="last", align_bytes=64)
+        for q in range(1, len(BATCHES)):
+            scales[q] = late[:, sum(widths[1:q]) : sum(widths[1 : q + 1])]
+        for q in range(1, len(BATCHES) - 1):
             quantize(q)
         quantize(len(BATCHES) - 1, calls=2)
         for i in range(len(GROUPS)):
-            empty(i, on_vector=(i >= 5))
+            empty(i, on_vector=(i == 5))
 
         ends = turns.tile([P, 2, T], F32, name="turn1", align_bytes=64)
         first, total = ends[:, 0, :], ends[:, 1, :]

@@ -99,10 +99,11 @@ def tile_moe_pre_lin_bias_kernel(tc, xT, w, b, gate, offs, pos1, pos2, out):
             for e in range(0, E, W_EXPERTS):
                 nc.sync.dma_start(w_raw[g][:, e : e + W_EXPERTS], w_rows[g][:, e : e + W_EXPERTS])
 
-        load_x(0, [0])
         nc.sync.dma_start(offs_sb[:], offs)
-        for lo, hi in HEAD:
+        for i, (lo, hi) in enumerate(HEAD):
             nc.sync.dma_start(gate_sb[:, lo:hi], gate[0:P, lo:hi])
+            if i == 0:
+                load_x(0, [0])
         load_x(0, [1, 2, 3])
         load_w(0)
         load_x(1, [0])

@@ -22,46 +22,25 @@ FP8X4 = mybir.dt.float8_e4m3fn_x4
 MULT = mybir.AluOpType.mult
 ADD = mybir.AluOpType.add
 IDENT = mybir.ActivationFunctionType.Identity
+COPY = mybir.ActivationFunctionType.Copy
 
-HEAD = [(0, 128), (128, 448), (448, 1024), (1024, 1536)]
-LAST = [(0, 768), (768, 1536)]
-GROUPS = [(0, 256), (256, 512), (512, 768), (768, 1024), (1024, 1280), (1280, 1408), (1408, 1536)]
-FETCH = [(0, 384), (384, 768)]
-OUT = [(0, 384), (384, 640), (640, 768)]
-WINDOW = S + PER_COL
-W_EXPERTS = 2
-
-BATCHES = [
-    [("w", 0, 0, 6), ("w", 1, 0, 2)],
-    [("x", 0, 0, 1024)],
-    [("w", 1, 2, 6), ("w", 2, 0, 4)],
-    [("x", 1, 0, 1024)],
-    [("x", 2, 0, 768), ("w", 2, 4, 6)],
-    [("x", 2, 768, 1280), ("x", 0, 1024, 1280), ("x", 1, 1024, 1280)],
-    [("x", 0, 1280, 1536), ("x", 1, 1280, 1536)],
-    [("x", 2, 1280, 1536)],
+OWN = [(0, 576)]
+UNITS = [
+    [(576, 1056), (1056, 1536)],
+    [(0, 512), (512, 1024), (1024, 1536)],
+    [(0, 512), (512, 1024), (1024, 1280), (1280, 1408), (1408, 1536)],
 ]
-HELD = 6
-
-
-def interleave(nc, dst, src):
-    nc.scalar.copy(
-        out=dst.rearrange("p (c i) t -> p c t i", i=PACK),
-        in_=src.rearrange("p t (c i) -> p c t i", i=PACK),
-    )
-
-
-def width(run):
-    kind, g, lo, hi = run
-    return (hi - lo) * (N if kind == "w" else 1)
+GROUPS = [(0, 256), (256, 512), (512, 768), (768, 1024), (1024, 1280), (1280, 1408), (1408, 1536)]
+OUT = [(0, 128), (128, 256), (256, 384), (384, 512), (512, 640), (640, 768)]
+STORES = [(0, 384), (384, 640), (640, 768)]
+W_EXPERTS = 2
 
 
 def tile_moe_pre_lin_bias_kernel(tc, xT, w, b, gate, offs, pos1, pos2, out):
     nc = tc.nc
     with ExitStack() as ctx:
         keep = ctx.enter_context(tc.tile_pool(name="keep", bufs=1))
-        windows = ctx.enter_context(tc.tile_pool(name="windows", bufs=2 * PACK))
-        turns = ctx.enter_context(tc.tile_pool(name="turns", bufs=1))
+        ring = ctx.enter_context(tc.tile_pool(name="ring", bufs=4))
         psum = ctx.enter_context(tc.psum_pool(name="psum", bufs=1))
 
         offs_sb = keep.tile([P, S // PER_COL], U16, name="offs_sb")
@@ -72,14 +51,12 @@ def tile_moe_pre_lin_bias_kernel(tc, xT, w, b, gate, offs, pos1, pos2, out):
         y = keep.tile([P, S], F32, name="y")
         acc = [psum.tile([P, hi - lo], F32, name=f"acc{i}") for i, (lo, hi) in enumerate(GROUPS)]
 
-        widths = [sum(width(run) for run in batch) for batch in BATCHES]
-        rounded = [keep.tile([P, n, PACK], BF16, name=f"rounded{q}", align_bytes=64) for q, n in enumerate(widths)]
-        scales = {0: keep.tile([P, widths[0]], U8, name="scales0", align_bytes=64)}
-        codes = {}
-        start = {}
-        for q, batch in enumerate(BATCHES):
-            for j, run in enumerate(batch):
-                start[run] = (q, sum(width(r) for r in batch[:j]))
+        x_round = [keep.tile([P, S * PACK], BF16, name=f"x_round{g}", align_bytes=64) for g in range(PASSES)]
+        w_round = [keep.tile([P, E * N * PACK], BF16, name=f"w_round{g}", align_bytes=64) for g in range(PASSES)]
+        x_codes = [keep.tile([P, S], U32, name=f"x_codes{g}", align_bytes=64) for g in range(PASSES)]
+        w_codes = [keep.tile([P, E * N], U32, name=f"w_codes{g}", align_bytes=64) for g in range(PASSES)]
+        x_scales = [keep.tile([P, S], U8, name=f"x_scales{g}", align_bytes=64) for g in range(PASSES)]
+        w_scales = [keep.tile([P, E * N], U8, name=f"w_scales{g}", align_bytes=64) for g in range(PASSES)]
 
         x_rows = xT.rearrange("(g p t) x -> g t p x", g=PASSES, t=PACK)
         w_rows = w.rearrange("e (g p t) n -> g p e t n", g=PASSES, t=PACK)
@@ -88,147 +65,151 @@ def tile_moe_pre_lin_bias_kernel(tc, xT, w, b, gate, offs, pos1, pos2, out):
 
         def load_x(g, planes):
             for t in planes:
-                if (g, t) == (PASSES - 1, PACK - 2):
-                    win[g, t] = turns.tile([P, WINDOW], F32, name="last", align_bytes=64)
-                else:
-                    win[g, t] = windows.tile([P, WINDOW], F32, name="win")
-                nc.sync.dma_start(win[g, t][:, 0:T], x_rows[g, t])
+                win[g, t] = keep.tile([P, T], F32, name=f"win{g}_{t}")
+                nc.sync.dma_start(win[g, t][:], x_rows[g, t])
 
         def load_w(g):
-            w_raw[g] = keep.tile([P, E, PACK, N], F32, name=f"w_raw{g}")
             for e in range(0, E, W_EXPERTS):
-                nc.sync.dma_start(w_raw[g][:, e : e + W_EXPERTS], w_rows[g][:, e : e + W_EXPERTS])
+                w_raw[g, e] = keep.tile([P, W_EXPERTS, PACK, N], F32, name=f"w_raw{g}_{e}")
+                nc.sync.dma_start(w_raw[g, e][:], w_rows[g][:, e : e + W_EXPERTS])
 
+        head = OWN[0][1]
         nc.sync.dma_start(offs_sb[:], offs)
-        for i, (lo, hi) in enumerate(HEAD):
-            nc.sync.dma_start(gate_sb[:, lo:hi], gate[0:P, lo:hi])
-            if i == 0:
-                load_x(0, [0])
+        load_x(0, [0])
+        nc.sync.dma_start(gate_sb[:, 0:head], gate[0:P, 0:head])
         load_x(0, [1, 2, 3])
+        nc.sync.dma_start(gate_sb[:, head:S], gate[0:P, head:S])
         load_w(0)
-        load_x(1, [0])
+        load_x(1, range(PACK))
         load_w(1)
-        load_x(1, [1, 2, 3])
         load_w(2)
+        load_x(2, range(PACK))
         nc.sync.dma_start(b_sb[:], b)
         nc.sync.dma_start(pos1_sb[:], pos1)
         nc.sync.dma_start(pos2_sb[:], pos2)
 
+        def listed(tile, lst, lo, hi):
+            return tile[:].indirect(lst[:, lo // PER_COL : hi // PER_COL])
+
         picked = {}
 
-        def gather(g, t, pieces):
-            if t == 0:
-                picked[g] = turns.tile([P, PACK, S], F32, name=f"turn{g % 2}", align_bytes=64)
-            for lo, hi in pieces:
-                nc.vector.tensor_tensor(
-                    picked[g][:, t, lo:hi],
-                    win[g, t][:].indirect(offs_sb[:, lo // PER_COL : hi // PER_COL]),
-                    gate_sb[:, lo:hi],
-                    MULT,
-                )
+        def pick(g, u):
+            lo, hi = UNITS[g][u]
+            picked[g, u] = ring.tile([P, PACK, hi - lo], F32, name="picked")
+            for t in range(PACK):
+                nc.scalar.activation(picked[g, u][:, t, :], listed(win[g, t], offs_sb, lo, hi), COPY)
 
-        def runs_of(kind, g):
-            return sorted(run for run in start if run[:2] == (kind, g))
+        def weigh(g, u):
+            lo, hi = UNITS[g][u]
+            pairs = (hi - lo) // 2
+            nc.vector.tensor_tensor(
+                x_round[g][:, lo * PACK : hi * PACK].rearrange("p (c i t) -> p c t i", i=2, t=PACK),
+                picked[g, u][:].rearrange("p t (c i) -> p c t i", i=2),
+                gate_sb[:, lo:hi].rearrange("p (c o i) -> p c o i", o=1, i=2).to_broadcast([P, pairs, PACK, 2]),
+                MULT,
+            )
 
-        def round_x(g):
-            for run in runs_of("x", g):
-                q, at = start[run]
-                interleave(nc, rounded[q][:, at : at + width(run), :], picked[g][:, :, run[2] : run[3]])
+        def own(g):
+            lo, hi = OWN[g]
+            picked[g] = keep.tile([P, PACK, hi - lo], F32, name=f"own{g}")
+            for t in range(PACK):
+                nc.vector.tensor_tensor(picked[g][:, t, :], listed(win[g, t], offs_sb, lo, hi), gate_sb[:, lo:hi], MULT)
+
+        def round_own(g):
+            lo, hi = OWN[g]
+            nc.vector.tensor_copy(
+                x_round[g][:, lo * PACK : hi * PACK].rearrange("p (c i t) -> p c t i", i=PACK, t=PACK),
+                picked[g][:].rearrange("p t (c i) -> p c t i", i=PACK),
+            )
 
         def round_w(g):
-            for run in runs_of("w", g):
-                q, at = start[run]
-                for e in range(run[2], run[3]):
-                    first = at + (e - run[2]) * N
-                    interleave(nc, rounded[q][:, first : first + N, :], w_raw[g][:, e])
+            for e in range(0, E, W_EXPERTS):
+                nc.vector.tensor_copy(
+                    w_round[g][:, e * N * PACK : (e + W_EXPERTS) * N * PACK].rearrange(
+                        "p (e c i t) -> p e c t i", e=W_EXPERTS, i=PACK, t=PACK
+                    ),
+                    w_raw[g, e][:].rearrange("p e t (c i) -> p e c t i", i=PACK),
+                )
 
-        def columns(kind, g, lo, n):
-            run = [r for r in runs_of(kind, g) if r[2] <= lo < r[3]][0]
-            q, at = start[run]
-            first = at + (lo - run[2]) * (N if kind == "w" else 1)
-            return q, slice(first, first + n)
-
+        done = {}
         passes_done = [0] * len(GROUPS)
-        multiplied = set()
-        done = [0] * len(BATCHES)
 
         def multiply_ready():
             for i, (lo, hi) in enumerate(GROUPS):
-                for g in range(PASSES):
-                    qw, w_cols = columns("w", g, lo // C, N)
-                    qx, x_cols = columns("x", g, lo, hi - lo)
-                    if (g, i) in multiplied or done[qw] < w_cols.stop or done[qx] < x_cols.stop:
-                        continue
+                g = passes_done[i]
+                while g < PASSES and done.get(("x", g), 0) >= hi and done.get(("w", g), 0) >= (lo // C + 1) * N:
+                    w_cols = slice(lo // C * N, (lo // C + 1) * N)
                     nc.tensor.matmul_mx(
                         out=acc[i][:],
-                        lhsT=codes[qw][:, w_cols].bitcast(FP8X4),
-                        lhsT_scale=scales[qw][:, w_cols],
-                        rhs=codes[qx][:, x_cols].bitcast(FP8X4),
-                        rhs_scale=scales[qx][:, x_cols],
-                        start=(passes_done[i] == 0),
-                        stop=(passes_done[i] == PASSES - 1),
+                        lhsT=w_codes[g][:, w_cols].bitcast(FP8X4),
+                        lhsT_scale=w_scales[g][:, w_cols],
+                        rhs=x_codes[g][:, lo:hi].bitcast(FP8X4),
+                        rhs_scale=x_scales[g][:, lo:hi],
+                        start=(g == 0),
+                        stop=(g == PASSES - 1),
                     )
-                    passes_done[i] += 1
-                    multiplied.add((g, i))
+                    g += 1
+                    passes_done[i] = g
+                    if g == PASSES:
+                        e = lo // C
+                        nc.scalar.activation(y[:, lo:hi], acc[i][:], IDENT, bias=b_sb[:, e : e + 1])
 
-        def quantize(q, calls=1):
-            if q == HELD:
-                codes[q] = turns.tile([P, widths[q]], U32, name="turn0", align_bytes=64)
-            else:
-                codes[q] = keep.tile([P, widths[q]], U32, name=f"codes{q}", align_bytes=64)
-            for c in range(calls):
-                cols = slice(c * widths[q] // calls, (c + 1) * widths[q] // calls)
+        def quantize(kind, g, *ends):
+            codes, scales, rounded = (x_codes, x_scales, x_round) if kind == "x" else (w_codes, w_scales, w_round)
+            for hi in ends:
+                lo = done.get((kind, g), 0)
                 nc.vector.quantize_mx(
-                    out=codes[q][:, cols].bitcast(FP8X4),
-                    scales=scales[q][:, cols],
-                    in_=rounded[q][:, cols, :].rearrange("p s t -> p (s t)"),
+                    out=codes[g][:, lo:hi].bitcast(FP8X4),
+                    scales=scales[g][:, lo:hi],
+                    in_=rounded[g][:, lo * PACK : hi * PACK],
                 )
-                done[q] = cols.stop
-                multiply_ready()
+                done[kind, g] = hi
 
-        def empty(i, on_vector):
-            lo, hi = GROUPS[i]
-            e = lo // C
-            if on_vector:
-                nc.vector.tensor_scalar(y[:, lo:hi], acc[i][:], b_sb[:, e : e + 1], None, ADD)
-            else:
-                nc.scalar.activation(y[:, lo:hi], acc[i][:], IDENT, bias=b_sb[:, e : e + 1])
+        order = [(g, u) for g in range(PASSES) for u in range(len(UNITS[g]))]
+        ahead = 4
+        for g, u in order[:ahead]:
+            pick(g, u)
 
-        whole = [(0, S)]
-        gather(0, 0, HEAD)
-        for t in range(1, PACK):
-            gather(0, t, whole)
-        load_x(2, range(PACK))
+        def step(n):
+            weigh(*order[n])
+            if n + ahead < len(order):
+                pick(*order[n + ahead])
+
+        own(0)
+        step(0)
+        round_own(0)
+        step(1)
         round_w(0)
+        quantize("x", 0, 1024, 1536)
+        quantize("w", 0, 512, 768)
+        step(2)
         round_w(1)
-        round_x(0)
+        quantize("x", 1, 512)
+        step(3)
+        quantize("w", 1, 512, 768)
         round_w(2)
-        gather(1, 0, whole)
-        gather(1, 1, whole)
-        quantize(0)
-        gather(1, 2, whole)
-        gather(1, 3, whole)
-        round_x(1)
-        for t in range(PACK - 1):
-            gather(2, t, whole)
-        gather(2, PACK - 1, LAST)
-        round_x(2)
-        late = turns.tile([P, sum(widths[1:])], U8, name="last", align_bytes=64)
-        for q in range(1, len(BATCHES)):
-            scales[q] = late[:, sum(widths[1:q]) : sum(widths[1 : q + 1])]
-        for q in range(1, len(BATCHES) - 1):
-            quantize(q)
-        quantize(len(BATCHES) - 1, calls=2)
-        for i in range(len(GROUPS)):
-            empty(i, on_vector=(i == 5))
+        quantize("x", 1, 1024)
+        step(4)
+        quantize("w", 2, 512, 768)
+        step(5)
+        quantize("x", 1, 1536)
+        step(6)
+        quantize("x", 2, 512)
+        step(7)
+        quantize("x", 2, 1024)
+        multiply_ready()
+        step(8)
+        quantize("x", 2, 1280)
+        step(9)
+        quantize("x", 2, 1408)
+        quantize("x", 2, 1536)
+        multiply_ready()
 
-        ends = turns.tile([P, 2, T], F32, name="turn1", align_bytes=64)
-        first, total = ends[:, 0, :], ends[:, 1, :]
-
-        for lo, hi in FETCH:
-            nc.vector.tensor_copy(first[:, lo:hi], y[:].indirect(pos1_sb[:, lo // PER_COL : hi // PER_COL]))
-        for i, (lo, hi) in enumerate(OUT):
-            nc.vector.tensor_tensor(
-                total[:, lo:hi], y[:].indirect(pos2_sb[:, lo // PER_COL : hi // PER_COL]), first[:, lo:hi], ADD
-            )
-            (nc.sync if i % 2 == 0 else nc.scalar).dma_start(out[:, lo:hi], total[:, lo:hi])
+        first = keep.tile([P, T], F32, name="first")
+        total = keep.tile([P, T], F32, name="total")
+        for lo, hi in OUT:
+            nc.scalar.activation(first[:, lo:hi], listed(y, pos1_sb, lo, hi), COPY)
+        for lo, hi in OUT:
+            nc.vector.tensor_tensor(total[:, lo:hi], listed(y, pos2_sb, lo, hi), first[:, lo:hi], ADD)
+        for lo, hi in STORES:
+            nc.sync.dma_start(out[:, lo:hi], total[:, lo:hi])

@@ -1,6 +1,7 @@
 from contextlib import ExitStack
 
 import concourse.mybir as mybir
+from concourse.masks import make_identity
 
 K, T, E, C, N = 1536, 768, 6, 256, 128
 S = E * C
@@ -9,6 +10,7 @@ PACK = 4
 K_PASS = P * PACK
 PASSES = K // K_PASS
 PER_COL = 16
+BANK = 512
 
 FLOPS = 2 * K * S * N
 BYTES = 4 * (K * T + E * K * N + N * E + S + N * T) + 2 * P * (S + 2 * T) // PER_COL
@@ -24,39 +26,42 @@ ADD = mybir.AluOpType.add
 IDENT = mybir.ActivationFunctionType.Identity
 COPY = mybir.ActivationFunctionType.Copy
 
-OWN = [(0, 576)]
+OWN = [(0, 768), (0, 128)]
 UNITS = [
-    [(576, 1056), (1056, 1536)],
-    [(0, 512), (512, 1024), (1024, 1536)],
-    [(0, 512), (512, 1024), (1024, 1280), (1280, 1408), (1408, 1536)],
+    [(768, 1536)],
+    [(128, 832), (832, 1536)],
+    [(0, 768), (768, 1280), (1280, 1536)],
 ]
 GROUPS = [(0, 256), (256, 512), (512, 768), (768, 1024), (1024, 1280), (1280, 1408), (1408, 1536)]
+BANKS = [(0, 512), (512, 1024), (1024, 1280), (1280, 1408), (1408, 1536)]
 OUT = [(0, 128), (128, 256), (256, 384), (384, 512), (512, 640), (640, 768)]
 STORES = [(0, 384), (384, 640), (640, 768)]
 W_EXPERTS = 2
+WINDOW = T + PER_COL
 
 
 def tile_moe_pre_lin_bias_kernel(tc, xT, w, b, gate, offs, pos1, pos2, out):
     nc = tc.nc
     with ExitStack() as ctx:
         keep = ctx.enter_context(tc.tile_pool(name="keep", bufs=1))
-        ring = ctx.enter_context(tc.tile_pool(name="ring", bufs=4))
+        ring = ctx.enter_context(tc.tile_pool(name="ring", bufs=3))
+        turns = ctx.enter_context(tc.tile_pool(name="turns", bufs=1))
         psum = ctx.enter_context(tc.psum_pool(name="psum", bufs=1))
 
         offs_sb = keep.tile([P, S // PER_COL], U16, name="offs_sb")
         pos1_sb = keep.tile([P, T // PER_COL], U16, name="pos1_sb")
         pos2_sb = keep.tile([P, T // PER_COL], U16, name="pos2_sb")
         b_sb = keep.tile([P, E], F32, name="b_sb")
-        gate_sb = keep.tile([P, S], F32, name="gate_sb")
+        gate_sb = keep.tile([P, S // BANK, BANK // P], F32, name="gate_sb")
+        ident = keep.tile([P, P], F32, name="ident")
         y = keep.tile([P, S], F32, name="y")
-        acc = [psum.tile([P, hi - lo], F32, name=f"acc{i}") for i, (lo, hi) in enumerate(GROUPS)]
+        spread = [psum.tile([P, BANK], F32, name=f"spread{j}") for j in range(S // BANK)]
+        acc = [psum.tile([P, hi - lo], F32, name=f"acc{i}") for i, (lo, hi) in enumerate(BANKS)]
 
         x_round = [keep.tile([P, S * PACK], BF16, name=f"x_round{g}", align_bytes=64) for g in range(PASSES)]
         w_round = [keep.tile([P, E * N * PACK], BF16, name=f"w_round{g}", align_bytes=64) for g in range(PASSES)]
         x_codes = [keep.tile([P, S], U32, name=f"x_codes{g}", align_bytes=64) for g in range(PASSES)]
         w_codes = [keep.tile([P, E * N], U32, name=f"w_codes{g}", align_bytes=64) for g in range(PASSES)]
-        x_scales = [keep.tile([P, S], U8, name=f"x_scales{g}", align_bytes=64) for g in range(PASSES)]
-        w_scales = [keep.tile([P, E * N], U8, name=f"w_scales{g}", align_bytes=64) for g in range(PASSES)]
 
         x_rows = xT.rearrange("(g p t) x -> g t p x", g=PASSES, t=PACK)
         w_rows = w.rearrange("e (g p t) n -> g p e t n", g=PASSES, t=PACK)
@@ -65,20 +70,21 @@ def tile_moe_pre_lin_bias_kernel(tc, xT, w, b, gate, offs, pos1, pos2, out):
 
         def load_x(g, planes):
             for t in planes:
-                win[g, t] = keep.tile([P, T], F32, name=f"win{g}_{t}")
-                nc.sync.dma_start(win[g, t][:], x_rows[g, t])
+                win[g, t] = keep.tile([P, WINDOW], F32, name=f"win{g}_{t}")
+                nc.sync.dma_start(win[g, t][:, 0:T], x_rows[g, t])
 
         def load_w(g):
             for e in range(0, E, W_EXPERTS):
-                w_raw[g, e] = keep.tile([P, W_EXPERTS, PACK, N], F32, name=f"w_raw{g}_{e}")
+                if (g, e) == (PASSES - 1, E - W_EXPERTS):
+                    w_raw[g, e] = turns.tile([P, W_EXPERTS, PACK, N], F32, name="last", align_bytes=64)
+                else:
+                    w_raw[g, e] = keep.tile([P, W_EXPERTS, PACK, N], F32, name=f"w_raw{g}_{e}")
                 nc.sync.dma_start(w_raw[g, e][:], w_rows[g][:, e : e + W_EXPERTS])
 
-        head = OWN[0][1]
         nc.sync.dma_start(offs_sb[:], offs)
         load_x(0, [0])
-        nc.sync.dma_start(gate_sb[:, 0:head], gate[0:P, 0:head])
+        nc.sync.dma_start(gate_sb[:], gate[0].rearrange("(j q r) -> q j r", q=P, r=BANK // P))
         load_x(0, [1, 2, 3])
-        nc.sync.dma_start(gate_sb[:, head:S], gate[0:P, head:S])
         load_w(0)
         load_x(1, range(PACK))
         load_w(1)
@@ -88,87 +94,101 @@ def tile_moe_pre_lin_bias_kernel(tc, xT, w, b, gate, offs, pos1, pos2, out):
         nc.sync.dma_start(pos1_sb[:], pos1)
         nc.sync.dma_start(pos2_sb[:], pos2)
 
+        make_identity(nc, ident[:])
+        for j in range(S // BANK):
+            for r in range(BANK // P):
+                nc.tensor.transpose(spread[j][:, r :: BANK // P], gate_sb[:, j, r : r + 1].to_broadcast([P, P]), ident[:])
+
         def listed(tile, lst, lo, hi):
             return tile[:].indirect(lst[:, lo // PER_COL : hi // PER_COL])
 
         picked = {}
 
-        def pick(g, u):
-            lo, hi = UNITS[g][u]
-            picked[g, u] = ring.tile([P, PACK, hi - lo], F32, name="picked")
+        def pick(g, lo, hi):
+            picked[g, lo] = ring.tile([P, PACK, hi - lo], F32, name="picked")
             for t in range(PACK):
-                nc.scalar.activation(picked[g, u][:, t, :], listed(win[g, t], offs_sb, lo, hi), COPY)
-
-        def weigh(g, u):
-            lo, hi = UNITS[g][u]
-            pairs = (hi - lo) // 2
-            nc.vector.tensor_tensor(
-                x_round[g][:, lo * PACK : hi * PACK].rearrange("p (c i t) -> p c t i", i=2, t=PACK),
-                picked[g, u][:].rearrange("p t (c i) -> p c t i", i=2),
-                gate_sb[:, lo:hi].rearrange("p (c o i) -> p c o i", o=1, i=2).to_broadcast([P, pairs, PACK, 2]),
-                MULT,
-            )
+                nc.scalar.activation(picked[g, lo][:, t, :], listed(win[g, t], offs_sb, lo, hi), COPY)
 
         def own(g):
             lo, hi = OWN[g]
-            picked[g] = keep.tile([P, PACK, hi - lo], F32, name=f"own{g}")
+            picked[g, lo] = keep.tile([P, PACK, hi - lo], F32, name=f"own{g}")
             for t in range(PACK):
-                nc.vector.tensor_tensor(picked[g][:, t, :], listed(win[g, t], offs_sb, lo, hi), gate_sb[:, lo:hi], MULT)
+                nc.vector.tensor_copy(picked[g, lo][:, t, :], listed(win[g, t], offs_sb, lo, hi))
 
-        def round_own(g):
-            lo, hi = OWN[g]
-            nc.vector.tensor_copy(
-                x_round[g][:, lo * PACK : hi * PACK].rearrange("p (c i t) -> p c t i", i=PACK, t=PACK),
-                picked[g][:].rearrange("p t (c i) -> p c t i", i=PACK),
-            )
-
-        def round_w(g):
-            for e in range(0, E, W_EXPERTS):
-                nc.vector.tensor_copy(
-                    w_round[g][:, e * N * PACK : (e + W_EXPERTS) * N * PACK].rearrange(
-                        "p (e c i t) -> p e c t i", e=W_EXPERTS, i=PACK, t=PACK
-                    ),
-                    w_raw[g, e][:].rearrange("p e t (c i) -> p e c t i", i=PACK),
+        def weigh(g, first, last):
+            cuts = [first] + [c for c in range(BANK, S, BANK) if first < c < last] + [last]
+            for lo, hi in zip(cuts, cuts[1:]):
+                j = lo // BANK
+                nc.vector.tensor_tensor(
+                    x_round[g][:, lo * PACK : hi * PACK].rearrange("p (c i t) -> p c t i", i=2, t=PACK),
+                    picked[g, first][:, :, lo - first : hi - first].rearrange("p t (c i) -> p c t i", i=2),
+                    spread[j][:, lo - j * BANK : hi - j * BANK]
+                    .rearrange("p (c o i) -> p c o i", o=1, i=2)
+                    .to_broadcast([P, (hi - lo) // 2, PACK, 2]),
+                    MULT,
                 )
+
+        for g in range(PASSES):
+            for e in range(0, E, W_EXPERTS):
+                nc.gpsimd.tensor_scalar(
+                    w_round[g][:, e * N * PACK : (e + W_EXPERTS) * N * PACK].rearrange(
+                        "p (e n t) -> p e n t", e=W_EXPERTS, t=PACK
+                    ),
+                    w_raw[g, e][:].rearrange("p e t n -> p e n t"),
+                    1.0,
+                    0.0,
+                    MULT,
+                    ADD,
+                )
+        scales = turns.tile([P, PASSES, S + E * N], U8, name="last", align_bytes=64)
+        x_scales = [scales[:, g, 0:S] for g in range(PASSES)]
+        w_scales = [scales[:, g, S:] for g in range(PASSES)]
 
         done = {}
         passes_done = [0] * len(GROUPS)
+        in_bank = [0] * len(BANKS)
 
         def multiply_ready():
             for i, (lo, hi) in enumerate(GROUPS):
+                k = [n for n, (a, z) in enumerate(BANKS) if a <= lo < z][0]
+                base, end = BANKS[k]
+                members = [m for m in GROUPS if base <= m[0] < end]
                 g = passes_done[i]
                 while g < PASSES and done.get(("x", g), 0) >= hi and done.get(("w", g), 0) >= (lo // C + 1) * N:
                     w_cols = slice(lo // C * N, (lo // C + 1) * N)
+                    in_bank[k] += 1
                     nc.tensor.matmul_mx(
-                        out=acc[i][:],
+                        out=acc[k][:, lo - base : hi - base],
                         lhsT=w_codes[g][:, w_cols].bitcast(FP8X4),
                         lhsT_scale=w_scales[g][:, w_cols],
                         rhs=x_codes[g][:, lo:hi].bitcast(FP8X4),
                         rhs_scale=x_scales[g][:, lo:hi],
-                        start=(g == 0),
-                        stop=(g == PASSES - 1),
+                        start=(in_bank[k] == 1),
+                        stop=(in_bank[k] == PASSES * len(members)),
                     )
                     g += 1
                     passes_done[i] = g
-                    if g == PASSES:
-                        e = lo // C
-                        nc.scalar.activation(y[:, lo:hi], acc[i][:], IDENT, bias=b_sb[:, e : e + 1])
+                    if in_bank[k] == PASSES * len(members):
+                        for a, z in members:
+                            e = a // C
+                            nc.scalar.activation(y[:, a:z], acc[k][:, a - base : z - base], IDENT, bias=b_sb[:, e : e + 1])
 
         def quantize(kind, g, *ends):
-            codes, scales, rounded = (x_codes, x_scales, x_round) if kind == "x" else (w_codes, w_scales, w_round)
+            codes, planes, rounded = (x_codes, x_scales, x_round) if kind == "x" else (w_codes, w_scales, w_round)
             for hi in ends:
                 lo = done.get((kind, g), 0)
                 nc.vector.quantize_mx(
                     out=codes[g][:, lo:hi].bitcast(FP8X4),
-                    scales=scales[g][:, lo:hi],
+                    scales=planes[g][:, lo:hi],
                     in_=rounded[g][:, lo * PACK : hi * PACK],
                 )
                 done[kind, g] = hi
+            multiply_ready()
 
-        order = [(g, u) for g in range(PASSES) for u in range(len(UNITS[g]))]
-        ahead = 4
-        for g, u in order[:ahead]:
-            pick(g, u)
+        order = [(g, lo, hi) for g in range(PASSES) for lo, hi in UNITS[g]]
+        ahead = 3
+        for unit in order[:ahead]:
+            pick(*unit)
 
         def step(n):
             weigh(*order[n])
@@ -176,34 +196,23 @@ def tile_moe_pre_lin_bias_kernel(tc, xT, w, b, gate, offs, pos1, pos2, out):
                 pick(*order[n + ahead])
 
         own(0)
+        weigh(0, *OWN[0])
         step(0)
-        round_own(0)
+        own(1)
         step(1)
-        round_w(0)
-        quantize("x", 0, 1024, 1536)
-        quantize("w", 0, 512, 768)
+        weigh(1, *OWN[1])
         step(2)
-        round_w(1)
-        quantize("x", 1, 512)
+        for g in range(PASSES):
+            quantize("w", g, 512, 768)
+        quantize("x", 0, 1024, 1536)
+        quantize("x", 1, 1024, 1536)
         step(3)
-        quantize("w", 1, 512, 768)
-        round_w(2)
-        quantize("x", 1, 1024)
         step(4)
-        quantize("w", 2, 512, 768)
+        quantize("x", 2, 512, 768)
         step(5)
-        quantize("x", 1, 1536)
-        step(6)
-        quantize("x", 2, 512)
-        step(7)
-        quantize("x", 2, 1024)
-        multiply_ready()
-        step(8)
         quantize("x", 2, 1280)
-        step(9)
         quantize("x", 2, 1408)
         quantize("x", 2, 1536)
-        multiply_ready()
 
         first = keep.tile([P, T], F32, name="first")
         total = keep.tile([P, T], F32, name="total")

@@ -26,25 +26,28 @@ ADD = mybir.AluOpType.add
 IDENT = mybir.ActivationFunctionType.Identity
 COPY = mybir.ActivationFunctionType.Copy
 
-OWN = [(0, 768), (0, 128)]
+OWN = 832
 UNITS = [
-    [(768, 1536)],
-    [(128, 832), (832, 1536)],
-    [(0, 768), (768, 1280), (1280, 1536)],
+    (0, OWN, 1536, "a"),
+    (1, 0, 896, "c"),
+    (1, 896, 1536, "b"),
+    (2, 0, 512, "c"),
+    (2, 512, 1024, "b"),
+    (2, 1024, 1408, "c"),
+    (2, 1408, 1536, "b"),
 ]
 GROUPS = [(0, 256), (256, 512), (512, 768), (768, 1024), (1024, 1280), (1280, 1408), (1408, 1536)]
 BANKS = [(0, 512), (512, 1024), (1024, 1280), (1280, 1408), (1408, 1536)]
-OUT = [(0, 128), (128, 256), (256, 384), (384, 512), (512, 640), (640, 768)]
+OUT = [(0, 128), (128, 384), (384, 640), (640, 768)]
 STORES = [(0, 384), (384, 640), (640, 768)]
 W_EXPERTS = 2
-WINDOW = T + PER_COL
+WINDOW = [848, 912, 768]
 
 
 def tile_moe_pre_lin_bias_kernel(tc, xT, w, b, gate, offs, pos1, pos2, out):
     nc = tc.nc
     with ExitStack() as ctx:
         keep = ctx.enter_context(tc.tile_pool(name="keep", bufs=1))
-        ring = ctx.enter_context(tc.tile_pool(name="ring", bufs=3))
         turns = ctx.enter_context(tc.tile_pool(name="turns", bufs=1))
         psum = ctx.enter_context(tc.psum_pool(name="psum", bufs=1))
 
@@ -58,8 +61,8 @@ def tile_moe_pre_lin_bias_kernel(tc, xT, w, b, gate, offs, pos1, pos2, out):
         spread = [psum.tile([P, BANK], F32, name=f"spread{j}") for j in range(S // BANK)]
         acc = [psum.tile([P, hi - lo], F32, name=f"acc{i}") for i, (lo, hi) in enumerate(BANKS)]
 
-        x_round = [keep.tile([P, S * PACK], BF16, name=f"x_round{g}", align_bytes=64) for g in range(PASSES)]
-        w_round = [keep.tile([P, E * N * PACK], BF16, name=f"w_round{g}", align_bytes=64) for g in range(PASSES)]
+        w_round = [turns.tile([P, E * N * PACK], BF16, name=f"round{g}", align_bytes=64) for g in range(PASSES)]
+        x_round = {}
         x_codes = [keep.tile([P, S], U32, name=f"x_codes{g}", align_bytes=64) for g in range(PASSES)]
         w_codes = [keep.tile([P, E * N], U32, name=f"w_codes{g}", align_bytes=64) for g in range(PASSES)]
 
@@ -70,23 +73,29 @@ def tile_moe_pre_lin_bias_kernel(tc, xT, w, b, gate, offs, pos1, pos2, out):
 
         def load_x(g, planes):
             for t in planes:
-                win[g, t] = keep.tile([P, WINDOW], F32, name=f"win{g}_{t}")
+                win[g, t] = keep.tile([P, WINDOW[g]], F32, name=f"win{g}_{t}")
                 nc.sync.dma_start(win[g, t][:, 0:T], x_rows[g, t])
 
-        def load_w(g):
-            for e in range(0, E, W_EXPERTS):
+        def load_w(g, first=0, end=E):
+            for e in range(first, end, W_EXPERTS):
                 if (g, e) == (PASSES - 1, E - W_EXPERTS):
                     w_raw[g, e] = turns.tile([P, W_EXPERTS, PACK, N], F32, name="last", align_bytes=64)
                 else:
                     w_raw[g, e] = keep.tile([P, W_EXPERTS, PACK, N], F32, name=f"w_raw{g}_{e}")
                 nc.sync.dma_start(w_raw[g, e][:], w_rows[g][:, e : e + W_EXPERTS])
 
+        warm = keep.tile([P, 2], F32, name="warm")
+        nc.vector.memset(warm[:, 0:1], 0.0)
+        nc.scalar.activation(warm[:, 1:2], warm[:, 0:1], IDENT)
+
         nc.sync.dma_start(offs_sb[:], offs)
         load_x(0, [0])
         nc.sync.dma_start(gate_sb[:], gate[0].rearrange("(j q r) -> q j r", q=P, r=BANK // P))
         load_x(0, [1, 2, 3])
-        load_w(0)
-        load_x(1, range(PACK))
+        load_w(0, 0, 4)
+        load_x(1, [0])
+        load_w(0, 4, 6)
+        load_x(1, [1, 2, 3])
         load_w(1)
         load_w(2)
         load_x(2, range(PACK))
@@ -104,23 +113,28 @@ def tile_moe_pre_lin_bias_kernel(tc, xT, w, b, gate, offs, pos1, pos2, out):
 
         picked = {}
 
-        def pick(g, lo, hi):
-            picked[g, lo] = ring.tile([P, PACK, hi - lo], F32, name="picked")
+        def pick(g, lo, hi, buffer):
+            picked[g, lo] = turns.tile([P, PACK, hi - lo], F32, name=buffer)
             for t in range(PACK):
                 nc.scalar.activation(picked[g, lo][:, t, :], listed(win[g, t], offs_sb, lo, hi), COPY)
 
-        def own(g):
-            lo, hi = OWN[g]
-            picked[g, lo] = keep.tile([P, PACK, hi - lo], F32, name=f"own{g}")
+        def own():
+            picked[0, 0] = turns.tile([P, PACK, OWN], F32, name="b")
             for t in range(PACK):
-                nc.vector.tensor_copy(picked[g, lo][:, t, :], listed(win[g, t], offs_sb, lo, hi))
+                nc.vector.tensor_copy(picked[0, 0][:, t, :], listed(win[0, t], offs_sb, 0, OWN))
 
-        def weigh(g, first, last):
-            cuts = [first] + [c for c in range(BANK, S, BANK) if first < c < last] + [last]
+        def rounded(kind, g, lo, hi):
+            if kind == "w":
+                return w_round[g][:, lo * PACK : hi * PACK]
+            first = max(a for p, a in x_round if p == g and a <= lo)
+            return x_round[g, first][:, (lo - first) * PACK : (hi - first) * PACK]
+
+        def weigh(g, first, last, cuts=()):
+            cuts = sorted({first, last, *cuts, *[c for c in range(BANK, S, BANK) if first < c < last]})
             for lo, hi in zip(cuts, cuts[1:]):
                 j = lo // BANK
                 nc.vector.tensor_tensor(
-                    x_round[g][:, lo * PACK : hi * PACK].rearrange("p (c i t) -> p c t i", i=2, t=PACK),
+                    rounded("x", g, lo, hi).rearrange("p (c i t) -> p c t i", i=2, t=PACK),
                     picked[g, first][:, :, lo - first : hi - first].rearrange("p t (c i) -> p c t i", i=2),
                     spread[j][:, lo - j * BANK : hi - j * BANK]
                     .rearrange("p (c o i) -> p c o i", o=1, i=2)
@@ -171,46 +185,52 @@ def tile_moe_pre_lin_bias_kernel(tc, xT, w, b, gate, offs, pos1, pos2, out):
                     if in_bank[k] == PASSES * len(members):
                         for a, z in members:
                             e = a // C
-                            nc.scalar.activation(y[:, a:z], acc[k][:, a - base : z - base], IDENT, bias=b_sb[:, e : e + 1])
+                            if k == len(BANKS) - 2:
+                                nc.vector.tensor_scalar(y[:, a:z], acc[k][:], b_sb[:, e : e + 1], None, ADD)
+                            else:
+                                nc.scalar.activation(
+                                    y[:, a:z], acc[k][:, a - base : z - base], IDENT, bias=b_sb[:, e : e + 1]
+                                )
 
         def quantize(kind, g, *ends):
-            codes, planes, rounded = (x_codes, x_scales, x_round) if kind == "x" else (w_codes, w_scales, w_round)
+            codes, planes = (x_codes, x_scales) if kind == "x" else (w_codes, w_scales)
             for hi in ends:
                 lo = done.get((kind, g), 0)
                 nc.vector.quantize_mx(
                     out=codes[g][:, lo:hi].bitcast(FP8X4),
                     scales=planes[g][:, lo:hi],
-                    in_=rounded[g][:, lo * PACK : hi * PACK],
+                    in_=rounded(kind, g, lo, hi),
                 )
                 done[kind, g] = hi
             multiply_ready()
 
-        order = [(g, lo, hi) for g in range(PASSES) for lo, hi in UNITS[g]]
-        ahead = 3
-        for unit in order[:ahead]:
-            pick(*unit)
-
-        def step(n):
-            weigh(*order[n])
-            if n + ahead < len(order):
-                pick(*order[n + ahead])
-
-        own(0)
-        weigh(0, *OWN[0])
-        step(0)
-        own(1)
-        step(1)
-        weigh(1, *OWN[1])
-        step(2)
+        x_round[0, 0] = keep.tile([P, S * PACK], BF16, name="x_round0", align_bytes=64)
+        x_round[1, 0] = keep.tile([P, 896 * PACK], BF16, name="x_round1", align_bytes=64)
+        x_round[2, 0] = keep.tile([P, S * PACK], BF16, name="x_round2", align_bytes=64)
+        pick(*UNITS[0])
+        pick(*UNITS[1])
+        own()
+        weigh(0, OWN, S)
+        weigh(0, 0, OWN)
+        pick(*UNITS[2])
+        weigh(1, 0, 896)
+        pick(*UNITS[3])
         for g in range(PASSES):
             quantize("w", g, 512, 768)
+        x_round[1, 896] = turns.tile([P, (S - 896) * PACK], BF16, name="round0", align_bytes=64)
+        weigh(1, 896, S)
+        pick(*UNITS[4])
         quantize("x", 0, 1024, 1536)
-        quantize("x", 1, 1024, 1536)
-        step(3)
-        step(4)
-        quantize("x", 2, 512, 768)
-        step(5)
+        weigh(2, 0, 512)
+        pick(*UNITS[5])
+        quantize("x", 1, 512, 896, 1408, 1536)
+        quantize("x", 2, 512)
+        weigh(2, 512, 1024, [768])
+        pick(*UNITS[6])
+        quantize("x", 2, 768, 1024)
+        weigh(2, 1024, 1408, [1280])
         quantize("x", 2, 1280)
+        weigh(2, 1408, 1536)
         quantize("x", 2, 1408)
         quantize("x", 2, 1536)
 

@@ -26,11 +26,11 @@ ADD = mybir.AluOpType.add
 IDENT = mybir.ActivationFunctionType.Identity
 COPY = mybir.ActivationFunctionType.Copy
 
-OWN = 832
+OWN = 960
 UNITS = [
     (0, OWN, 1536, "a"),
-    (1, 0, 896, "c"),
-    (1, 896, 1536, "b"),
+    (1, 0, 1024, "c"),
+    (1, 1024, 1536, "b"),
     (2, 0, 512, "c"),
     (2, 512, 1024, "b"),
     (2, 1024, 1408, "c"),
@@ -38,10 +38,9 @@ UNITS = [
 ]
 GROUPS = [(0, 256), (256, 512), (512, 768), (768, 1024), (1024, 1280), (1280, 1408), (1408, 1536)]
 BANKS = [(0, 512), (512, 1024), (1024, 1280), (1280, 1408), (1408, 1536)]
-OUT = [(0, 128), (128, 384), (384, 640), (640, 768)]
-STORES = [(0, 384), (384, 640), (640, 768)]
+OUT = [(0, 256), (256, 512), (512, 768)]
 W_EXPERTS = 2
-WINDOW = [848, 912, 768]
+WINDOW = [976, 1040, 768]
 
 
 def tile_moe_pre_lin_bias_kernel(tc, xT, w, b, gate, offs, pos1, pos2, out):
@@ -92,9 +91,9 @@ def tile_moe_pre_lin_bias_kernel(tc, xT, w, b, gate, offs, pos1, pos2, out):
         load_x(0, [0])
         nc.sync.dma_start(gate_sb[:], gate[0].rearrange("(j q r) -> q j r", q=P, r=BANK // P))
         load_x(0, [1, 2, 3])
-        load_w(0, 0, 4)
+        load_w(0, 0, 2)
         load_x(1, [0])
-        load_w(0, 4, 6)
+        load_w(0, 2, 6)
         load_x(1, [1, 2, 3])
         load_w(1)
         load_w(2)
@@ -185,7 +184,7 @@ def tile_moe_pre_lin_bias_kernel(tc, xT, w, b, gate, offs, pos1, pos2, out):
                     if in_bank[k] == PASSES * len(members):
                         for a, z in members:
                             e = a // C
-                            if k == len(BANKS) - 2:
+                            if k == len(BANKS) - 1:
                                 nc.vector.tensor_scalar(y[:, a:z], acc[k][:], b_sb[:, e : e + 1], None, ADD)
                             else:
                                 nc.scalar.activation(
@@ -205,7 +204,7 @@ def tile_moe_pre_lin_bias_kernel(tc, xT, w, b, gate, offs, pos1, pos2, out):
             multiply_ready()
 
         x_round[0, 0] = keep.tile([P, S * PACK], BF16, name="x_round0", align_bytes=64)
-        x_round[1, 0] = keep.tile([P, 896 * PACK], BF16, name="x_round1", align_bytes=64)
+        x_round[1, 0] = keep.tile([P, 1024 * PACK], BF16, name="x_round1", align_bytes=64)
         x_round[2, 0] = keep.tile([P, S * PACK], BF16, name="x_round2", align_bytes=64)
         pick(*UNITS[0])
         pick(*UNITS[1])
@@ -213,17 +212,17 @@ def tile_moe_pre_lin_bias_kernel(tc, xT, w, b, gate, offs, pos1, pos2, out):
         weigh(0, OWN, S)
         weigh(0, 0, OWN)
         pick(*UNITS[2])
-        weigh(1, 0, 896)
+        weigh(1, 0, 1024)
         pick(*UNITS[3])
         for g in range(PASSES):
             quantize("w", g, 512, 768)
-        x_round[1, 896] = turns.tile([P, (S - 896) * PACK], BF16, name="round0", align_bytes=64)
-        weigh(1, 896, S)
+        x_round[1, 1024] = turns.tile([P, (S - 1024) * PACK], BF16, name="round0", align_bytes=64)
+        weigh(1, 1024, S)
         pick(*UNITS[4])
         quantize("x", 0, 1024, 1536)
         weigh(2, 0, 512)
         pick(*UNITS[5])
-        quantize("x", 1, 512, 896, 1408, 1536)
+        quantize("x", 1, 1024, 1536)
         quantize("x", 2, 512)
         weigh(2, 512, 1024, [768])
         pick(*UNITS[6])
@@ -236,9 +235,13 @@ def tile_moe_pre_lin_bias_kernel(tc, xT, w, b, gate, offs, pos1, pos2, out):
 
         first = keep.tile([P, T], F32, name="first")
         total = keep.tile([P, T], F32, name="total")
+        last_lo, last_hi = OUT[-1]
+        second = keep.tile([P, last_hi - last_lo], F32, name="second")
+        nc.vector.tensor_copy(second[:], listed(y, pos2_sb, last_lo, last_hi))
         for lo, hi in OUT:
             nc.scalar.activation(first[:, lo:hi], listed(y, pos1_sb, lo, hi), COPY)
-        for lo, hi in OUT:
+        for lo, hi in OUT[:-1]:
             nc.vector.tensor_tensor(total[:, lo:hi], listed(y, pos2_sb, lo, hi), first[:, lo:hi], ADD)
-        for lo, hi in STORES:
             nc.sync.dma_start(out[:, lo:hi], total[:, lo:hi])
+        nc.vector.tensor_tensor(total[:, last_lo:last_hi], second[:], first[:, last_lo:last_hi], ADD)
+        nc.sync.dma_start(out[:, last_lo:last_hi], total[:, last_lo:last_hi])

@@ -26,21 +26,22 @@ ADD = mybir.AluOpType.add
 IDENT = mybir.ActivationFunctionType.Identity
 COPY = mybir.ActivationFunctionType.Copy
 
-OWN = 960
+OWN = 1088
 UNITS = [
     (0, OWN, 1536, "a"),
     (1, 0, 1024, "c"),
     (1, 1024, 1536, "b"),
-    (2, 0, 512, "c"),
-    (2, 512, 1024, "b"),
-    (2, 1024, 1408, "c"),
-    (2, 1408, 1536, "b"),
+    (2, 0, 512, "a"),
+    (2, 512, 1024, "round0"),
+    (2, 1024, 1408, "b"),
+    (2, 1408, 1536, "a"),
 ]
 GROUPS = [(0, 256), (256, 512), (512, 768), (768, 1024), (1024, 1280), (1280, 1408), (1408, 1536)]
 BANKS = [(0, 512), (512, 1024), (1024, 1280), (1280, 1408), (1408, 1536)]
 OUT = [(0, 256), (256, 512), (512, 768)]
 W_EXPERTS = 2
-WINDOW = [976, 1040, 768]
+PIECE = W_EXPERTS * PACK * N * 4
+WINDOW = [1104, 1040, 768]
 
 
 def tile_moe_pre_lin_bias_kernel(tc, xT, w, b, gate, offs, pos1, pos2, out):
@@ -48,6 +49,7 @@ def tile_moe_pre_lin_bias_kernel(tc, xT, w, b, gate, offs, pos1, pos2, out):
     with ExitStack() as ctx:
         keep = ctx.enter_context(tc.tile_pool(name="keep", bufs=1))
         turns = ctx.enter_context(tc.tile_pool(name="turns", bufs=1))
+        laid = ctx.enter_context(tc.tile_pool(name="laid", bufs=1))
         psum = ctx.enter_context(tc.psum_pool(name="psum", bufs=1))
 
         offs_sb = keep.tile([P, S // PER_COL], U16, name="offs_sb")
@@ -55,15 +57,16 @@ def tile_moe_pre_lin_bias_kernel(tc, xT, w, b, gate, offs, pos1, pos2, out):
         pos2_sb = keep.tile([P, T // PER_COL], U16, name="pos2_sb")
         b_sb = keep.tile([P, E], F32, name="b_sb")
         gate_sb = keep.tile([P, S // BANK, BANK // P], F32, name="gate_sb")
+        gate_rows = keep.tile([P, S - OWN], F32, name="gate_rows")
         ident = keep.tile([P, P], F32, name="ident")
         y = keep.tile([P, S], F32, name="y")
         spread = [psum.tile([P, BANK], F32, name=f"spread{j}") for j in range(S // BANK)]
         acc = [psum.tile([P, hi - lo], F32, name=f"acc{i}") for i, (lo, hi) in enumerate(BANKS)]
 
-        w_round = [turns.tile([P, E * N * PACK], BF16, name=f"round{g}", align_bytes=64) for g in range(PASSES)]
+        w_round = {g: turns.tile([P, E * N * PACK], BF16, name=f"round{g}", align_bytes=64) for g in range(PASSES - 1)}
         x_round = {}
-        x_codes = [keep.tile([P, S], U32, name=f"x_codes{g}", align_bytes=64) for g in range(PASSES)]
-        w_codes = [keep.tile([P, E * N], U32, name=f"w_codes{g}", align_bytes=64) for g in range(PASSES)]
+        codes = {}
+        scales = {}
 
         x_rows = xT.rearrange("(g p t) x -> g t p x", g=PASSES, t=PACK)
         w_rows = w.rearrange("e (g p t) n -> g p e t n", g=PASSES, t=PACK)
@@ -77,8 +80,10 @@ def tile_moe_pre_lin_bias_kernel(tc, xT, w, b, gate, offs, pos1, pos2, out):
 
         def load_w(g, first=0, end=E):
             for e in range(first, end, W_EXPERTS):
-                if (g, e) == (PASSES - 1, E - W_EXPERTS):
-                    w_raw[g, e] = turns.tile([P, W_EXPERTS, PACK, N], F32, name="last", align_bytes=64)
+                if g > 0 and e == E - W_EXPERTS:
+                    w_raw[g, e] = laid.tile(
+                        [P, W_EXPERTS, PACK, N], F32, name=f"last{g}", align_bytes=64, offset=(g - 1) * PIECE
+                    )
                 else:
                     w_raw[g, e] = keep.tile([P, W_EXPERTS, PACK, N], F32, name=f"w_raw{g}_{e}")
                 nc.sync.dma_start(w_raw[g, e][:], w_rows[g][:, e : e + W_EXPERTS])
@@ -93,11 +98,13 @@ def tile_moe_pre_lin_bias_kernel(tc, xT, w, b, gate, offs, pos1, pos2, out):
         load_x(0, [1, 2, 3])
         load_w(0, 0, 2)
         load_x(1, [0])
-        load_w(0, 2, 6)
+        nc.sync.dma_start(gate_rows[:], gate[0:P, OWN:S])
         load_x(1, [1, 2, 3])
-        load_w(1)
-        load_w(2)
+        load_w(0, 2, 6)
+        load_w(1, 0, 4)
         load_x(2, range(PACK))
+        load_w(1, 4, 6)
+        load_w(2)
         nc.sync.dma_start(b_sb[:], b)
         nc.sync.dma_start(pos1_sb[:], pos1)
         nc.sync.dma_start(pos2_sb[:], pos2)
@@ -113,12 +120,12 @@ def tile_moe_pre_lin_bias_kernel(tc, xT, w, b, gate, offs, pos1, pos2, out):
         picked = {}
 
         def pick(g, lo, hi, buffer):
-            picked[g, lo] = turns.tile([P, PACK, hi - lo], F32, name=buffer)
+            picked[g, lo] = turns.tile([P, PACK, hi - lo], F32, name=buffer, align_bytes=64)
             for t in range(PACK):
                 nc.scalar.activation(picked[g, lo][:, t, :], listed(win[g, t], offs_sb, lo, hi), COPY)
 
         def own():
-            picked[0, 0] = turns.tile([P, PACK, OWN], F32, name="b")
+            picked[0, 0] = turns.tile([P, PACK, OWN], F32, name="b", align_bytes=64)
             for t in range(PACK):
                 nc.vector.tensor_copy(picked[0, 0][:, t, :], listed(win[0, t], offs_sb, 0, OWN))
 
@@ -141,8 +148,20 @@ def tile_moe_pre_lin_bias_kernel(tc, xT, w, b, gate, offs, pos1, pos2, out):
                     MULT,
                 )
 
-        for g in range(PASSES):
+        x_round[0, 0] = turns.tile([P, S * PACK], BF16, name="x_round0", align_bytes=64)
+        pick(*UNITS[0])
+
+        def round_w(g):
             for e in range(0, E, W_EXPERTS):
+                if (g, e) == (0, W_EXPERTS):
+                    nc.gpsimd.tensor_tensor(
+                        rounded("x", 0, OWN, S).rearrange("p (c i t) -> p c t i", i=2, t=PACK),
+                        picked[0, OWN][:].rearrange("p t (c i) -> p c t i", i=2),
+                        gate_rows[:]
+                        .rearrange("p (c o i) -> p c o i", o=1, i=2)
+                        .to_broadcast([P, (S - OWN) // 2, PACK, 2]),
+                        MULT,
+                    )
                 nc.gpsimd.tensor_scalar(
                     w_round[g][:, e * N * PACK : (e + W_EXPERTS) * N * PACK].rearrange(
                         "p (e n t) -> p e n t", e=W_EXPERTS, t=PACK
@@ -153,13 +172,17 @@ def tile_moe_pre_lin_bias_kernel(tc, xT, w, b, gate, offs, pos1, pos2, out):
                     MULT,
                     ADD,
                 )
-        scales = turns.tile([P, PASSES, S + E * N], U8, name="last", align_bytes=64)
-        x_scales = [scales[:, g, 0:S] for g in range(PASSES)]
-        w_scales = [scales[:, g, S:] for g in range(PASSES)]
+
+        round_w(0)
+        round_w(1)
 
         done = {}
         passes_done = [0] * len(GROUPS)
         in_bank = [0] * len(BANKS)
+
+        def columns(tiles, kind, g, lo, hi):
+            first = max(a for k, p, a in tiles if (k, p) == (kind, g) and a <= lo)
+            return tiles[kind, g, first][:, lo - first : hi - first]
 
         def multiply_ready():
             for i, (lo, hi) in enumerate(GROUPS):
@@ -168,14 +191,14 @@ def tile_moe_pre_lin_bias_kernel(tc, xT, w, b, gate, offs, pos1, pos2, out):
                 members = [m for m in GROUPS if base <= m[0] < end]
                 g = passes_done[i]
                 while g < PASSES and done.get(("x", g), 0) >= hi and done.get(("w", g), 0) >= (lo // C + 1) * N:
-                    w_cols = slice(lo // C * N, (lo // C + 1) * N)
+                    e = lo // C
                     in_bank[k] += 1
                     nc.tensor.matmul_mx(
                         out=acc[k][:, lo - base : hi - base],
-                        lhsT=w_codes[g][:, w_cols].bitcast(FP8X4),
-                        lhsT_scale=w_scales[g][:, w_cols],
-                        rhs=x_codes[g][:, lo:hi].bitcast(FP8X4),
-                        rhs_scale=x_scales[g][:, lo:hi],
+                        lhsT=columns(codes, "w", g, e * N, (e + 1) * N).bitcast(FP8X4),
+                        lhsT_scale=columns(scales, "w", g, e * N, (e + 1) * N),
+                        rhs=columns(codes, "x", g, lo, hi).bitcast(FP8X4),
+                        rhs_scale=columns(scales, "x", g, lo, hi),
                         start=(in_bank[k] == 1),
                         stop=(in_bank[k] == PASSES * len(members)),
                     )
@@ -191,41 +214,49 @@ def tile_moe_pre_lin_bias_kernel(tc, xT, w, b, gate, offs, pos1, pos2, out):
                                     y[:, a:z], acc[k][:, a - base : z - base], IDENT, bias=b_sb[:, e : e + 1]
                                 )
 
+        free = [0]
+
         def quantize(kind, g, *ends):
-            codes, planes = (x_codes, x_scales) if kind == "x" else (w_codes, w_scales)
             for hi in ends:
                 lo = done.get((kind, g), 0)
+                name = f"{kind}{g}_{lo}"
+                codes[kind, g, lo] = keep.tile([P, hi - lo], U32, name=f"codes_{name}", align_bytes=64)
+                scales[kind, g, lo] = laid.tile([P, hi - lo], U8, name=f"scales_{name}", align_bytes=64, offset=free[0])
+                free[0] += hi - lo
                 nc.vector.quantize_mx(
-                    out=codes[g][:, lo:hi].bitcast(FP8X4),
-                    scales=planes[g][:, lo:hi],
+                    out=codes[kind, g, lo][:].bitcast(FP8X4),
+                    scales=scales[kind, g, lo][:],
                     in_=rounded(kind, g, lo, hi),
                 )
                 done[kind, g] = hi
             multiply_ready()
 
-        x_round[0, 0] = keep.tile([P, S * PACK], BF16, name="x_round0", align_bytes=64)
         x_round[1, 0] = keep.tile([P, 1024 * PACK], BF16, name="x_round1", align_bytes=64)
-        x_round[2, 0] = keep.tile([P, S * PACK], BF16, name="x_round2", align_bytes=64)
-        pick(*UNITS[0])
         pick(*UNITS[1])
         own()
-        weigh(0, OWN, S)
         weigh(0, 0, OWN)
         pick(*UNITS[2])
         weigh(1, 0, 1024)
         pick(*UNITS[3])
-        for g in range(PASSES):
-            quantize("w", g, 512, 768)
-        x_round[1, 1024] = turns.tile([P, (S - 1024) * PACK], BF16, name="round0", align_bytes=64)
-        weigh(1, 1024, S)
+        quantize("w", 0, 512, 768)
         pick(*UNITS[4])
+        quantize("w", 1, 512, 768)
         quantize("x", 0, 1024, 1536)
-        weigh(2, 0, 512)
+        w_round[2] = turns.tile([P, E * N * PACK], BF16, name="x_round0", align_bytes=64)
+        round_w(2)
+        free[0] = PIECE
+        held = turns.tile([P, (S - 1024 + 512) * PACK], BF16, name="round1", align_bytes=64)
+        x_round[1, 1024] = held[:, 0 : (S - 1024) * PACK]
+        x_round[2, 0] = held[:, (S - 1024) * PACK :]
+        weigh(1, 1024, S)
         pick(*UNITS[5])
+        weigh(2, 0, 512)
+        pick(*UNITS[6])
+        quantize("w", 2, 512, 768)
+        x_round[2, 512] = turns.tile([P, (S - 512) * PACK], BF16, name="x_round0", align_bytes=64)
         quantize("x", 1, 1024, 1536)
         quantize("x", 2, 512)
         weigh(2, 512, 1024, [768])
-        pick(*UNITS[6])
         quantize("x", 2, 768, 1024)
         weigh(2, 1024, 1408, [1280])
         quantize("x", 2, 1280)

@@ -40,7 +40,8 @@ GROUPS = [(0, 256), (256, 512), (512, 768), (768, 1024), (1024, 1280), (1280, 14
 BANKS = [(0, 512), (512, 1024), (1024, 1280), (1280, 1408), (1408, 1536)]
 OUT = [(0, 256), (256, 512), (512, 768)]
 W_EXPERTS = 2
-PIECE = W_EXPERTS * PACK * N * 4
+W_RUNS = [(0, 0, 2), (0, 2, 6), (1, 0, 6), (2, 0, 2), (2, 2, 6)]
+HOLDS = {(1, 0, 6): 0, (2, 2, 6): E * PACK * N * 4}
 WINDOW = [1104, 1040, 768]
 
 
@@ -78,15 +79,15 @@ def tile_moe_pre_lin_bias_kernel(tc, xT, w, b, gate, offs, pos1, pos2, out):
                 win[g, t] = keep.tile([P, WINDOW[g]], F32, name=f"win{g}_{t}")
                 nc.sync.dma_start(win[g, t][:, 0:T], x_rows[g, t])
 
-        def load_w(g, first=0, end=E):
+        def load_w(run):
+            g, first, end = run
+            shape = [P, end - first, PACK, N]
+            if run in HOLDS:
+                w_raw[run] = laid.tile(shape, F32, name=f"w_raw{g}_{first}", align_bytes=64, offset=HOLDS[run])
+            else:
+                w_raw[run] = keep.tile(shape, F32, name=f"w_raw{g}_{first}")
             for e in range(first, end, W_EXPERTS):
-                if g > 0 and e == E - W_EXPERTS:
-                    w_raw[g, e] = laid.tile(
-                        [P, W_EXPERTS, PACK, N], F32, name=f"last{g}", align_bytes=64, offset=(g - 1) * PIECE
-                    )
-                else:
-                    w_raw[g, e] = keep.tile([P, W_EXPERTS, PACK, N], F32, name=f"w_raw{g}_{e}")
-                nc.sync.dma_start(w_raw[g, e][:], w_rows[g][:, e : e + W_EXPERTS])
+                nc.sync.dma_start(w_raw[run][:, e - first : e - first + W_EXPERTS], w_rows[g][:, e : e + W_EXPERTS])
 
         warm = keep.tile([P, 2], F32, name="warm")
         nc.vector.memset(warm[:, 0:1], 0.0)
@@ -96,15 +97,15 @@ def tile_moe_pre_lin_bias_kernel(tc, xT, w, b, gate, offs, pos1, pos2, out):
         load_x(0, [0])
         nc.sync.dma_start(gate_sb[:], gate[0].rearrange("(j q r) -> q j r", q=P, r=BANK // P))
         load_x(0, [1, 2, 3])
-        load_w(0, 0, 2)
-        load_x(1, [0])
         nc.sync.dma_start(gate_rows[:], gate[0:P, OWN:S])
-        load_x(1, [1, 2, 3])
-        load_w(0, 2, 6)
-        load_w(1, 0, 4)
+        load_x(1, [0, 1])
+        load_w(W_RUNS[0])
+        load_x(1, [2, 3])
+        load_w(W_RUNS[1])
+        load_w(W_RUNS[2])
         load_x(2, range(PACK))
-        load_w(1, 4, 6)
-        load_w(2)
+        load_w(W_RUNS[3])
+        load_w(W_RUNS[4])
         nc.sync.dma_start(b_sb[:], b)
         nc.sync.dma_start(pos1_sb[:], pos1)
         nc.sync.dma_start(pos2_sb[:], pos2)
@@ -151,30 +152,25 @@ def tile_moe_pre_lin_bias_kernel(tc, xT, w, b, gate, offs, pos1, pos2, out):
         x_round[0, 0] = turns.tile([P, S * PACK], BF16, name="x_round0", align_bytes=64)
         pick(*UNITS[0])
 
-        def round_w(g):
-            for e in range(0, E, W_EXPERTS):
-                if (g, e) == (0, W_EXPERTS):
-                    nc.gpsimd.tensor_tensor(
-                        rounded("x", 0, OWN, S).rearrange("p (c i t) -> p c t i", i=2, t=PACK),
-                        picked[0, OWN][:].rearrange("p t (c i) -> p c t i", i=2),
-                        gate_rows[:]
-                        .rearrange("p (c o i) -> p c o i", o=1, i=2)
-                        .to_broadcast([P, (S - OWN) // 2, PACK, 2]),
-                        MULT,
-                    )
-                nc.gpsimd.tensor_scalar(
-                    w_round[g][:, e * N * PACK : (e + W_EXPERTS) * N * PACK].rearrange(
-                        "p (e n t) -> p e n t", e=W_EXPERTS, t=PACK
-                    ),
-                    w_raw[g, e][:].rearrange("p e t n -> p e n t"),
-                    1.0,
-                    0.0,
-                    MULT,
-                    ADD,
-                )
+        def round_w(run):
+            g, first, end = run
+            nc.gpsimd.tensor_scalar(
+                w_round[g][:, first * N * PACK : end * N * PACK].rearrange("p (e n t) -> p e n t", n=N, t=PACK),
+                w_raw[run][:].rearrange("p e t n -> p e n t"),
+                1.0,
+                0.0,
+                MULT,
+                ADD,
+            )
 
-        round_w(0)
-        round_w(1)
+        nc.gpsimd.tensor_tensor(
+            rounded("x", 0, OWN, S).rearrange("p (s t) -> p s t", t=PACK),
+            picked[0, OWN][:].rearrange("p t s -> p s t"),
+            gate_rows[:].rearrange("p (s o) -> p s o", o=1).to_broadcast([P, S - OWN, PACK]),
+            MULT,
+        )
+        for run in W_RUNS[:3]:
+            round_w(run)
 
         done = {}
         passes_done = [0] * len(GROUPS)
@@ -243,8 +239,9 @@ def tile_moe_pre_lin_bias_kernel(tc, xT, w, b, gate, offs, pos1, pos2, out):
         quantize("w", 1, 512, 768)
         quantize("x", 0, 1024, 1536)
         w_round[2] = turns.tile([P, E * N * PACK], BF16, name="x_round0", align_bytes=64)
-        round_w(2)
-        free[0] = PIECE
+        for run in W_RUNS[3:]:
+            round_w(run)
+        free[0] = HOLDS[W_RUNS[-1]]
         held = turns.tile([P, (S - 1024 + 512) * PACK], BF16, name="round1", align_bytes=64)
         x_round[1, 1024] = held[:, 0 : (S - 1024) * PACK]
         x_round[2, 0] = held[:, (S - 1024) * PACK :]

@@ -30,11 +30,12 @@ OWN = 1088
 UNITS = [
     (0, OWN, 1536, "a"),
     (1, 0, 1024, "c"),
-    (1, 1024, 1536, "b"),
+    (1, 1024, 1536, "d"),
     (2, 0, 512, "a"),
     (2, 512, 1024, "round0"),
-    (2, 1024, 1408, "b"),
-    (2, 1408, 1536, "a"),
+    (2, 1024, 1280, "d"),
+    (2, 1280, 1472, "a"),
+    (2, 1472, 1536, "round1"),
 ]
 GROUPS = [(0, 256), (256, 512), (512, 768), (768, 1024), (1024, 1280), (1280, 1408), (1408, 1536)]
 BANKS = [(0, 512), (512, 1024), (1024, 1280), (1280, 1408), (1408, 1536)]
@@ -84,6 +85,8 @@ def tile_moe_pre_lin_bias_kernel(tc, xT, w, b, gate, offs, pos1, pos2, out):
             shape = [P, end - first, PACK, N]
             if run in HOLDS:
                 w_raw[run] = laid.tile(shape, F32, name=f"w_raw{g}_{first}", align_bytes=64, offset=HOLDS[run])
+            elif run == W_RUNS[0]:
+                w_raw[run] = turns.tile(shape, F32, name="d", align_bytes=64)
             else:
                 w_raw[run] = keep.tile(shape, F32, name=f"w_raw{g}_{first}")
             for e in range(first, end, W_EXPERTS):
@@ -98,9 +101,8 @@ def tile_moe_pre_lin_bias_kernel(tc, xT, w, b, gate, offs, pos1, pos2, out):
         nc.sync.dma_start(gate_sb[:], gate[0].rearrange("(j q r) -> q j r", q=P, r=BANK // P))
         load_x(0, [1, 2, 3])
         nc.sync.dma_start(gate_rows[:], gate[0:P, OWN:S])
-        load_x(1, [0, 1])
+        load_x(1, range(PACK))
         load_w(W_RUNS[0])
-        load_x(1, [2, 3])
         load_w(W_RUNS[1])
         load_w(W_RUNS[2])
         load_x(2, range(PACK))
@@ -203,7 +205,7 @@ def tile_moe_pre_lin_bias_kernel(tc, xT, w, b, gate, offs, pos1, pos2, out):
                     if in_bank[k] == PASSES * len(members):
                         for a, z in members:
                             e = a // C
-                            if k == len(BANKS) - 1:
+                            if k >= 3:
                                 nc.vector.tensor_scalar(y[:, a:z], acc[k][:], b_sb[:, e : e + 1], None, ADD)
                             else:
                                 nc.scalar.activation(
@@ -253,11 +255,13 @@ def tile_moe_pre_lin_bias_kernel(tc, xT, w, b, gate, offs, pos1, pos2, out):
         x_round[2, 512] = turns.tile([P, (S - 512) * PACK], BF16, name="x_round0", align_bytes=64)
         quantize("x", 1, 1024, 1536)
         quantize("x", 2, 512)
+        pick(*UNITS[7])
         weigh(2, 512, 1024, [768])
-        quantize("x", 2, 768, 1024)
-        weigh(2, 1024, 1408, [1280])
-        quantize("x", 2, 1280)
-        weigh(2, 1408, 1536)
+        quantize("x", 2, 768)
+        weigh(2, 1024, 1280)
+        quantize("x", 2, 1024, 1280)
+        weigh(2, 1280, 1472)
+        weigh(2, 1472, 1536)
         quantize("x", 2, 1408)
         quantize("x", 2, 1536)
 
@@ -271,5 +275,8 @@ def tile_moe_pre_lin_bias_kernel(tc, xT, w, b, gate, offs, pos1, pos2, out):
         for lo, hi in OUT[:-1]:
             nc.vector.tensor_tensor(total[:, lo:hi], listed(y, pos2_sb, lo, hi), first[:, lo:hi], ADD)
             nc.sync.dma_start(out[:, lo:hi], total[:, lo:hi])
-        nc.vector.tensor_tensor(total[:, last_lo:last_hi], second[:], first[:, last_lo:last_hi], ADD)
-        nc.sync.dma_start(out[:, last_lo:last_hi], total[:, last_lo:last_hi])
+        for lo in range(last_lo, last_hi, P):
+            nc.vector.tensor_tensor(
+                total[:, lo : lo + P], second[:, lo - last_lo : lo - last_lo + P], first[:, lo : lo + P], ADD
+            )
+            nc.sync.dma_start(out[:, lo : lo + P], total[:, lo : lo + P])

@@ -26,24 +26,25 @@ ADD = mybir.AluOpType.add
 IDENT = mybir.ActivationFunctionType.Identity
 COPY = mybir.ActivationFunctionType.Copy
 
-OWN = 1088
+OWN = 1024
+FIRST = 896
 UNITS = [
     (0, OWN, 1536, "a"),
-    (1, 0, 1024, "c"),
-    (1, 1024, 1536, "d"),
+    (1, 0, FIRST, "c"),
+    (1, FIRST, 1536, "d"),
     (2, 0, 512, "a"),
     (2, 512, 1024, "round0"),
-    (2, 1024, 1280, "d"),
-    (2, 1280, 1472, "a"),
-    (2, 1472, 1536, "round1"),
+    (2, 1024, 1344, "d"),
+    (2, 1344, 1536, "a"),
 ]
 GROUPS = [(0, 256), (256, 512), (512, 768), (768, 1024), (1024, 1280), (1280, 1408), (1408, 1536)]
 BANKS = [(0, 512), (512, 1024), (1024, 1280), (1280, 1408), (1408, 1536)]
 OUT = [(0, 256), (256, 512), (512, 768)]
 W_EXPERTS = 2
-W_RUNS = [(0, 0, 2), (0, 2, 6), (1, 0, 6), (2, 0, 2), (2, 2, 6)]
-HOLDS = {(1, 0, 6): 0, (2, 2, 6): E * PACK * N * 4}
-WINDOW = [1104, 1040, 768]
+W_RUNS = [(0, 2), (2, 3), (3, 6), (6, 10), (10, 16), (16, 18)]
+BLOCK = PACK * N * 4
+HOLDS = {(6, 10): 0, (10, 16): 7 * BLOCK}
+WINDOW = [1040, 912, 768]
 
 
 def tile_moe_pre_lin_bias_kernel(tc, xT, w, b, gate, offs, pos1, pos2, out):
@@ -65,8 +66,7 @@ def tile_moe_pre_lin_bias_kernel(tc, xT, w, b, gate, offs, pos1, pos2, out):
         spread = [psum.tile([P, BANK], F32, name=f"spread{j}") for j in range(S // BANK)]
         acc = [psum.tile([P, hi - lo], F32, name=f"acc{i}") for i, (lo, hi) in enumerate(BANKS)]
 
-        w_round = {g: turns.tile([P, E * N * PACK], BF16, name=f"round{g}", align_bytes=64) for g in range(PASSES - 1)}
-        x_round = {}
+        rounds = {("w", 0, 0): turns.tile([P, 10 * N * PACK], BF16, name="round0", align_bytes=64)}
         codes = {}
         scales = {}
 
@@ -81,16 +81,17 @@ def tile_moe_pre_lin_bias_kernel(tc, xT, w, b, gate, offs, pos1, pos2, out):
                 nc.sync.dma_start(win[g, t][:, 0:T], x_rows[g, t])
 
         def load_w(run):
-            g, first, end = run
+            first, end = run
             shape = [P, end - first, PACK, N]
             if run in HOLDS:
-                w_raw[run] = laid.tile(shape, F32, name=f"w_raw{g}_{first}", align_bytes=64, offset=HOLDS[run])
-            elif run == W_RUNS[0]:
+                w_raw[run] = laid.tile(shape, F32, name=f"w_raw{first}", align_bytes=64, offset=HOLDS[run])
+            elif run == W_RUNS[1]:
                 w_raw[run] = turns.tile(shape, F32, name="d", align_bytes=64)
             else:
-                w_raw[run] = keep.tile(shape, F32, name=f"w_raw{g}_{first}")
-            for e in range(first, end, W_EXPERTS):
-                nc.sync.dma_start(w_raw[run][:, e - first : e - first + W_EXPERTS], w_rows[g][:, e : e + W_EXPERTS])
+                w_raw[run] = keep.tile(shape, F32, name=f"w_raw{first}")
+            cuts = sorted({first, end, *range(first + first % W_EXPERTS, end, W_EXPERTS)})
+            for lo, hi in zip(cuts, cuts[1:]):
+                nc.sync.dma_start(w_raw[run][:, lo - first : hi - first], w_rows[lo // E][:, lo % E : lo % E + hi - lo])
 
         warm = keep.tile([P, 2], F32, name="warm")
         nc.vector.memset(warm[:, 0:1], 0.0)
@@ -100,14 +101,15 @@ def tile_moe_pre_lin_bias_kernel(tc, xT, w, b, gate, offs, pos1, pos2, out):
         load_x(0, [0])
         nc.sync.dma_start(gate_sb[:], gate[0].rearrange("(j q r) -> q j r", q=P, r=BANK // P))
         load_x(0, [1, 2, 3])
-        nc.sync.dma_start(gate_rows[:], gate[0:P, OWN:S])
-        load_x(1, range(PACK))
         load_w(W_RUNS[0])
-        load_w(W_RUNS[1])
-        load_w(W_RUNS[2])
+        load_x(1, [0])
+        nc.sync.dma_start(gate_rows[:], gate[0:P, OWN:S])
+        load_x(1, [1, 2, 3])
+        for run in W_RUNS[1:4]:
+            load_w(run)
         load_x(2, range(PACK))
-        load_w(W_RUNS[3])
-        load_w(W_RUNS[4])
+        for run in W_RUNS[4:]:
+            load_w(run)
         nc.sync.dma_start(b_sb[:], b)
         nc.sync.dma_start(pos1_sb[:], pos1)
         nc.sync.dma_start(pos2_sb[:], pos2)
@@ -132,11 +134,12 @@ def tile_moe_pre_lin_bias_kernel(tc, xT, w, b, gate, offs, pos1, pos2, out):
             for t in range(PACK):
                 nc.vector.tensor_copy(picked[0, 0][:, t, :], listed(win[0, t], offs_sb, 0, OWN))
 
+        def columns(tiles, kind, g, lo, hi, per=1):
+            first = max(a for k, p, a in tiles if (k, p) == (kind, g) and a <= lo)
+            return tiles[kind, g, first][:, (lo - first) * per : (hi - first) * per]
+
         def rounded(kind, g, lo, hi):
-            if kind == "w":
-                return w_round[g][:, lo * PACK : hi * PACK]
-            first = max(a for p, a in x_round if p == g and a <= lo)
-            return x_round[g, first][:, (lo - first) * PACK : (hi - first) * PACK]
+            return columns(rounds, kind, g, lo, hi, PACK)
 
         def weigh(g, first, last, cuts=()):
             cuts = sorted({first, last, *cuts, *[c for c in range(BANK, S, BANK) if first < c < last]})
@@ -151,13 +154,13 @@ def tile_moe_pre_lin_bias_kernel(tc, xT, w, b, gate, offs, pos1, pos2, out):
                     MULT,
                 )
 
-        x_round[0, 0] = turns.tile([P, S * PACK], BF16, name="x_round0", align_bytes=64)
+        rounds["x", 0, 0] = turns.tile([P, S * PACK], BF16, name="x_round0", align_bytes=64)
         pick(*UNITS[0])
 
         def round_w(run):
-            g, first, end = run
+            first, end = run
             nc.gpsimd.tensor_scalar(
-                w_round[g][:, first * N * PACK : end * N * PACK].rearrange("p (e n t) -> p e n t", n=N, t=PACK),
+                rounded("w", 0, first * N, end * N).rearrange("p (e n t) -> p e n t", n=N, t=PACK),
                 w_raw[run][:].rearrange("p e t n -> p e n t"),
                 1.0,
                 0.0,
@@ -165,22 +168,19 @@ def tile_moe_pre_lin_bias_kernel(tc, xT, w, b, gate, offs, pos1, pos2, out):
                 ADD,
             )
 
+        round_w(W_RUNS[0])
         nc.gpsimd.tensor_tensor(
             rounded("x", 0, OWN, S).rearrange("p (s t) -> p s t", t=PACK),
             picked[0, OWN][:].rearrange("p t s -> p s t"),
             gate_rows[:].rearrange("p (s o) -> p s o", o=1).to_broadcast([P, S - OWN, PACK]),
             MULT,
         )
-        for run in W_RUNS[:3]:
+        for run in W_RUNS[1:4]:
             round_w(run)
 
         done = {}
         passes_done = [0] * len(GROUPS)
         in_bank = [0] * len(BANKS)
-
-        def columns(tiles, kind, g, lo, hi):
-            first = max(a for k, p, a in tiles if (k, p) == (kind, g) and a <= lo)
-            return tiles[kind, g, first][:, lo - first : hi - first]
 
         def multiply_ready():
             for i, (lo, hi) in enumerate(GROUPS):
@@ -188,13 +188,13 @@ def tile_moe_pre_lin_bias_kernel(tc, xT, w, b, gate, offs, pos1, pos2, out):
                 base, end = BANKS[k]
                 members = [m for m in GROUPS if base <= m[0] < end]
                 g = passes_done[i]
-                while g < PASSES and done.get(("x", g), 0) >= hi and done.get(("w", g), 0) >= (lo // C + 1) * N:
-                    e = lo // C
+                while g < PASSES and done.get(("x", g), 0) >= hi and done.get(("w", 0), 0) >= (g * E + lo // C + 1) * N:
+                    j = g * E + lo // C
                     in_bank[k] += 1
                     nc.tensor.matmul_mx(
                         out=acc[k][:, lo - base : hi - base],
-                        lhsT=columns(codes, "w", g, e * N, (e + 1) * N).bitcast(FP8X4),
-                        lhsT_scale=columns(scales, "w", g, e * N, (e + 1) * N),
+                        lhsT=columns(codes, "w", 0, j * N, (j + 1) * N).bitcast(FP8X4),
+                        lhsT_scale=columns(scales, "w", 0, j * N, (j + 1) * N),
                         rhs=columns(codes, "x", g, lo, hi).bitcast(FP8X4),
                         rhs_scale=columns(scales, "x", g, lo, hi),
                         start=(in_bank[k] == 1),
@@ -205,7 +205,7 @@ def tile_moe_pre_lin_bias_kernel(tc, xT, w, b, gate, offs, pos1, pos2, out):
                     if in_bank[k] == PASSES * len(members):
                         for a, z in members:
                             e = a // C
-                            if k >= 3:
+                            if k == len(BANKS) - 1:
                                 nc.vector.tensor_scalar(y[:, a:z], acc[k][:], b_sb[:, e : e + 1], None, ADD)
                             else:
                                 nc.scalar.activation(
@@ -215,53 +215,54 @@ def tile_moe_pre_lin_bias_kernel(tc, xT, w, b, gate, offs, pos1, pos2, out):
         free = [0]
 
         def quantize(kind, g, *ends):
+            first = done.get((kind, g), 0)
+            name = f"{kind}{g}_{first}"
+            width = ends[-1] - first
+            codes[kind, g, first] = keep.tile([P, width], U32, name=f"codes_{name}", align_bytes=64)
+            scales[kind, g, first] = laid.tile([P, width], U8, name=f"scales_{name}", align_bytes=64, offset=free[0])
+            free[0] += width
             for hi in ends:
                 lo = done.get((kind, g), 0)
-                name = f"{kind}{g}_{lo}"
-                codes[kind, g, lo] = keep.tile([P, hi - lo], U32, name=f"codes_{name}", align_bytes=64)
-                scales[kind, g, lo] = laid.tile([P, hi - lo], U8, name=f"scales_{name}", align_bytes=64, offset=free[0])
-                free[0] += hi - lo
                 nc.vector.quantize_mx(
-                    out=codes[kind, g, lo][:].bitcast(FP8X4),
-                    scales=scales[kind, g, lo][:],
+                    out=columns(codes, kind, g, lo, hi).bitcast(FP8X4),
+                    scales=columns(scales, kind, g, lo, hi),
                     in_=rounded(kind, g, lo, hi),
                 )
                 done[kind, g] = hi
             multiply_ready()
 
-        x_round[1, 0] = keep.tile([P, 1024 * PACK], BF16, name="x_round1", align_bytes=64)
+        rounds["x", 1, 0] = keep.tile([P, FIRST * PACK], BF16, name="x_round1", align_bytes=64)
         pick(*UNITS[1])
         own()
         weigh(0, 0, OWN)
         pick(*UNITS[2])
-        weigh(1, 0, 1024)
+        weigh(1, 0, FIRST)
         pick(*UNITS[3])
-        quantize("w", 0, 512, 768)
+        quantize("w", 0, 8 * N, 10 * N)
         pick(*UNITS[4])
-        quantize("w", 1, 512, 768)
         quantize("x", 0, 1024, 1536)
-        w_round[2] = turns.tile([P, E * N * PACK], BF16, name="x_round0", align_bytes=64)
-        for run in W_RUNS[3:]:
-            round_w(run)
-        free[0] = HOLDS[W_RUNS[-1]]
-        held = turns.tile([P, (S - 1024 + 512) * PACK], BF16, name="round1", align_bytes=64)
-        x_round[1, 1024] = held[:, 0 : (S - 1024) * PACK]
-        x_round[2, 0] = held[:, (S - 1024) * PACK :]
-        weigh(1, 1024, S)
+        rounds["w", 0, 10 * N] = turns.tile([P, 6 * N * PACK], BF16, name="x_round0", align_bytes=64)
+        round_w(W_RUNS[4])
+        free[0] = HOLDS[W_RUNS[4]]
+        held = laid.tile([P, (S - FIRST + 512) * PACK], BF16, name="held", align_bytes=64, offset=2 * BLOCK)
+        rounds["x", 1, FIRST] = held[:, 0 : (S - FIRST) * PACK]
+        rounds["x", 2, 0] = held[:, (S - FIRST) * PACK :]
+        weigh(1, FIRST, S)
         pick(*UNITS[5])
         weigh(2, 0, 512)
         pick(*UNITS[6])
-        quantize("w", 2, 512, 768)
-        x_round[2, 512] = turns.tile([P, (S - 512) * PACK], BF16, name="x_round0", align_bytes=64)
-        quantize("x", 1, 1024, 1536)
+        quantize("w", 0, 14 * N, 16 * N)
+        rounds["x", 2, 512] = turns.tile([P, (S - 512) * PACK], BF16, name="x_round0", align_bytes=64)
+        quantize("x", 1, 512, FIRST, FIRST + 512, S)
         quantize("x", 2, 512)
-        pick(*UNITS[7])
+        rounds["w", 0, 16 * N] = laid.tile([P, 2 * N * PACK], BF16, name="w_last", align_bytes=64, offset=2 * BLOCK)
+        round_w(W_RUNS[5])
         weigh(2, 512, 1024, [768])
-        quantize("x", 2, 768)
-        weigh(2, 1024, 1280)
-        quantize("x", 2, 1024, 1280)
-        weigh(2, 1280, 1472)
-        weigh(2, 1472, 1536)
+        quantize("w", 0, 18 * N)
+        quantize("x", 2, 768, 1024)
+        weigh(2, 1024, 1344, [1280])
+        quantize("x", 2, 1280)
+        weigh(2, 1344, 1536, [1408])
         quantize("x", 2, 1408)
         quantize("x", 2, 1536)
 
@@ -275,8 +276,5 @@ def tile_moe_pre_lin_bias_kernel(tc, xT, w, b, gate, offs, pos1, pos2, out):
         for lo, hi in OUT[:-1]:
             nc.vector.tensor_tensor(total[:, lo:hi], listed(y, pos2_sb, lo, hi), first[:, lo:hi], ADD)
             nc.sync.dma_start(out[:, lo:hi], total[:, lo:hi])
-        for lo in range(last_lo, last_hi, P):
-            nc.vector.tensor_tensor(
-                total[:, lo : lo + P], second[:, lo - last_lo : lo - last_lo + P], first[:, lo : lo + P], ADD
-            )
-            nc.sync.dma_start(out[:, lo : lo + P], total[:, lo : lo + P])
+        nc.vector.tensor_tensor(total[:, last_lo:last_hi], second[:], first[:, last_lo:last_hi], ADD)
+        nc.sync.dma_start(out[:, last_lo:last_hi], total[:, last_lo:last_hi])

@@ -26,7 +26,8 @@ ADD = mybir.AluOpType.add
 IDENT = mybir.ActivationFunctionType.Identity
 COPY = mybir.ActivationFunctionType.Copy
 
-OWN = 1024
+OWN = 1056
+KEPT = 992
 FIRST = 896
 UNITS = [
     (0, OWN, 1536, "a"),
@@ -41,10 +42,10 @@ GROUPS = [(0, 256), (256, 512), (512, 768), (768, 1024), (1024, 1280), (1280, 14
 BANKS = [(0, 512), (512, 1024), (1024, 1280), (1280, 1408), (1408, 1536)]
 OUT = [(0, 256), (256, 512), (512, 768)]
 W_EXPERTS = 2
-W_RUNS = [(0, 2), (2, 3), (3, 6), (6, 10), (10, 16), (16, 18)]
+W_RUNS = [(0, 1), (1, 2), (2, 6), (6, 10), (10, 16), (16, 18)]
 BLOCK = PACK * N * 4
 HOLDS = {(6, 10): 0, (10, 16): 7 * BLOCK}
-WINDOW = [1040, 912, 768]
+WINDOW = [1072, 912, 768]
 
 
 def tile_moe_pre_lin_bias_kernel(tc, xT, w, b, gate, offs, pos1, pos2, out):
@@ -60,7 +61,7 @@ def tile_moe_pre_lin_bias_kernel(tc, xT, w, b, gate, offs, pos1, pos2, out):
         pos2_sb = keep.tile([P, T // PER_COL], U16, name="pos2_sb")
         b_sb = keep.tile([P, E], F32, name="b_sb")
         gate_sb = keep.tile([P, S // BANK, BANK // P], F32, name="gate_sb")
-        gate_rows = keep.tile([P, S - OWN], F32, name="gate_rows")
+        gate_rows = keep.tile([P, S - KEPT], F32, name="gate_rows")
         ident = keep.tile([P, P], F32, name="ident")
         y = keep.tile([P, S], F32, name="y")
         spread = [psum.tile([P, BANK], F32, name=f"spread{j}") for j in range(S // BANK)]
@@ -103,7 +104,7 @@ def tile_moe_pre_lin_bias_kernel(tc, xT, w, b, gate, offs, pos1, pos2, out):
         load_x(0, [1, 2, 3])
         load_w(W_RUNS[0])
         load_x(1, [0])
-        nc.sync.dma_start(gate_rows[:], gate[0:P, OWN:S])
+        nc.sync.dma_start(gate_rows[:], gate[0:P, KEPT:S])
         load_x(1, [1, 2, 3])
         for run in W_RUNS[1:4]:
             load_w(run)
@@ -168,14 +169,20 @@ def tile_moe_pre_lin_bias_kernel(tc, xT, w, b, gate, offs, pos1, pos2, out):
                 ADD,
             )
 
+        def weigh_beside(first, lo, hi):
+            nc.gpsimd.tensor_tensor(
+                rounded("x", 0, lo, hi).rearrange("p (s t) -> p s t", t=PACK),
+                picked[0, first][:, :, lo - first : hi - first].rearrange("p t s -> p s t"),
+                gate_rows[:, lo - KEPT : hi - KEPT].rearrange("p (s o) -> p s o", o=1).to_broadcast([P, hi - lo, PACK]),
+                MULT,
+            )
+
+        own()
         round_w(W_RUNS[0])
-        nc.gpsimd.tensor_tensor(
-            rounded("x", 0, OWN, S).rearrange("p (s t) -> p s t", t=PACK),
-            picked[0, OWN][:].rearrange("p t s -> p s t"),
-            gate_rows[:].rearrange("p (s o) -> p s o", o=1).to_broadcast([P, S - OWN, PACK]),
-            MULT,
-        )
-        for run in W_RUNS[1:4]:
+        weigh_beside(OWN, OWN, S)
+        round_w(W_RUNS[1])
+        weigh_beside(0, KEPT, OWN)
+        for run in W_RUNS[2:4]:
             round_w(run)
 
         done = {}
@@ -233,8 +240,7 @@ def tile_moe_pre_lin_bias_kernel(tc, xT, w, b, gate, offs, pos1, pos2, out):
 
         rounds["x", 1, 0] = keep.tile([P, FIRST * PACK], BF16, name="x_round1", align_bytes=64)
         pick(*UNITS[1])
-        own()
-        weigh(0, 0, OWN)
+        weigh(0, 0, KEPT)
         pick(*UNITS[2])
         weigh(1, 0, FIRST)
         pick(*UNITS[3])
@@ -257,9 +263,9 @@ def tile_moe_pre_lin_bias_kernel(tc, xT, w, b, gate, offs, pos1, pos2, out):
         quantize("x", 2, 512)
         rounds["w", 0, 16 * N] = laid.tile([P, 2 * N * PACK], BF16, name="w_last", align_bytes=64, offset=2 * BLOCK)
         round_w(W_RUNS[5])
-        weigh(2, 512, 1024, [768])
+        weigh(2, 512, 1024)
         quantize("w", 0, 18 * N)
-        quantize("x", 2, 768, 1024)
+        quantize("x", 2, 1024)
         weigh(2, 1024, 1344, [1280])
         quantize("x", 2, 1280)
         weigh(2, 1344, 1536, [1408])

@@ -26,33 +26,25 @@ ADD = mybir.AluOpType.add
 IDENT = mybir.ActivationFunctionType.Identity
 COPY = mybir.ActivationFunctionType.Copy
 
-OWN = 1056
-KEPT = 992
-FIRST = 896
-UNITS = [
-    (0, OWN, 1536, "a"),
-    (1, 0, FIRST, "c"),
-    (1, FIRST, 1536, "d"),
-    (2, 0, 512, "a"),
-    (2, 512, 1024, "round0"),
-    (2, 1024, 1344, "d"),
-    (2, 1344, 1536, "a"),
-]
-GROUPS = [(0, 256), (256, 512), (512, 768), (768, 1024), (1024, 1280), (1280, 1408), (1408, 1536)]
-BANKS = [(0, 512), (512, 1024), (1024, 1280), (1280, 1408), (1408, 1536)]
+OWN = 1152
+KEPT = 1120
+MID = 1488
+LATE = 1216
+FINAL = 304
+GROUPS = [(512, 768), (768, 1024), (1024, 1280), (1280, 1536), (0, 256), (384, 512), (256, 384)]
+BANKS = [(512, 1024), (1024, 1536), (0, 256), (384, 512), (256, 384)]
 OUT = [(0, 256), (256, 512), (512, 768)]
 W_EXPERTS = 2
-W_RUNS = [(0, 1), (1, 2), (2, 6), (6, 10), (10, 16), (16, 18)]
-BLOCK = PACK * N * 4
-HOLDS = {(6, 10): 0, (10, 16): 7 * BLOCK}
-WINDOW = [1072, 912, 768]
+W_RUNS = [(0, 2), (2, 6), (6, 10), (10, 14), (14, 18)]
+WINDOW = [OWN + PER_COL, S + PER_COL, 1024 + PER_COL]
+KIB = 1024
+AT_X0, AT_RAW2, AT_W0, AT_RAW4, AT_OWN, AT_ALL = 0, 18 * KIB, 26 * KIB, 34 * KIB, 42 * KIB, 61 * KIB
 
 
 def tile_moe_pre_lin_bias_kernel(tc, xT, w, b, gate, offs, pos1, pos2, out):
     nc = tc.nc
     with ExitStack() as ctx:
         keep = ctx.enter_context(tc.tile_pool(name="keep", bufs=1))
-        turns = ctx.enter_context(tc.tile_pool(name="turns", bufs=1))
         laid = ctx.enter_context(tc.tile_pool(name="laid", bufs=1))
         psum = ctx.enter_context(tc.psum_pool(name="psum", bufs=1))
 
@@ -61,15 +53,18 @@ def tile_moe_pre_lin_bias_kernel(tc, xT, w, b, gate, offs, pos1, pos2, out):
         pos2_sb = keep.tile([P, T // PER_COL], U16, name="pos2_sb")
         b_sb = keep.tile([P, E], F32, name="b_sb")
         gate_sb = keep.tile([P, S // BANK, BANK // P], F32, name="gate_sb")
-        gate_rows = keep.tile([P, S - KEPT], F32, name="gate_rows")
+        gate_rows = {lo: keep.tile([P, hi - lo], F32, name=f"gate_rows{lo}") for lo, hi in ((KEPT, OWN), (OWN, S), (C, FINAL))}
         ident = keep.tile([P, P], F32, name="ident")
         y = keep.tile([P, S], F32, name="y")
         spread = [psum.tile([P, BANK], F32, name=f"spread{j}") for j in range(S // BANK)]
         acc = [psum.tile([P, hi - lo], F32, name=f"acc{i}") for i, (lo, hi) in enumerate(BANKS)]
+        codes = {g: keep.tile([P, S], U32, name=f"codes_x{g}", align_bytes=64) for g in range(PASSES)}
+        codes["w"] = keep.tile([P, PASSES * E * N], U32, name="codes_w", align_bytes=64)
 
-        rounds = {("w", 0, 0): turns.tile([P, 10 * N * PACK], BF16, name="round0", align_bytes=64)}
-        codes = {}
-        scales = {}
+        def place(shape, dtype, name, where):
+            if where is None:
+                return keep.tile(shape, dtype, name=name, align_bytes=64)
+            return laid.tile(shape, dtype, name=name, align_bytes=64, offset=where)
 
         x_rows = xT.rearrange("(g p t) x -> g t p x", g=PASSES, t=PACK)
         w_rows = w.rearrange("e (g p t) n -> g p e t n", g=PASSES, t=PACK)
@@ -81,36 +76,34 @@ def tile_moe_pre_lin_bias_kernel(tc, xT, w, b, gate, offs, pos1, pos2, out):
                 win[g, t] = keep.tile([P, WINDOW[g]], F32, name=f"win{g}_{t}")
                 nc.sync.dma_start(win[g, t][:, 0:T], x_rows[g, t])
 
-        def load_w(run):
+        def load_w(run, where):
             first, end = run
-            shape = [P, end - first, PACK, N]
-            if run in HOLDS:
-                w_raw[run] = laid.tile(shape, F32, name=f"w_raw{first}", align_bytes=64, offset=HOLDS[run])
-            elif run == W_RUNS[1]:
-                w_raw[run] = turns.tile(shape, F32, name="d", align_bytes=64)
-            else:
-                w_raw[run] = keep.tile(shape, F32, name=f"w_raw{first}")
-            cuts = sorted({first, end, *range(first + first % W_EXPERTS, end, W_EXPERTS)})
-            for lo, hi in zip(cuts, cuts[1:]):
-                nc.sync.dma_start(w_raw[run][:, lo - first : hi - first], w_rows[lo // E][:, lo % E : lo % E + hi - lo])
+            w_raw[run] = place([P, end - first, PACK, N], F32, f"w_raw{first}", where)
+            for lo in range(first, end, W_EXPERTS):
+                hi = lo + W_EXPERTS
+                nc.sync.dma_start(w_raw[run][:, lo - first : hi - first], w_rows[lo // E][:, lo % E : lo % E + W_EXPERTS])
 
         warm = keep.tile([P, 2], F32, name="warm")
         nc.vector.memset(warm[:, 0:1], 0.0)
         nc.scalar.activation(warm[:, 1:2], warm[:, 0:1], IDENT)
 
         nc.sync.dma_start(offs_sb[:], offs)
-        load_x(0, [0])
-        nc.sync.dma_start(gate_sb[:], gate[0].rearrange("(j q r) -> q j r", q=P, r=BANK // P))
-        load_x(0, [1, 2, 3])
-        load_w(W_RUNS[0])
+        load_x(0, range(PACK))
         load_x(1, [0])
-        nc.sync.dma_start(gate_rows[:], gate[0:P, KEPT:S])
-        load_x(1, [1, 2, 3])
-        for run in W_RUNS[1:4]:
-            load_w(run)
-        load_x(2, range(PACK))
-        for run in W_RUNS[4:]:
-            load_w(run)
+        nc.sync.dma_start(gate_rows[OWN][:], gate[0:P, OWN:S])
+        nc.sync.dma_start(gate_sb[:], gate[0].rearrange("(j q r) -> q j r", q=P, r=BANK // P))
+        load_w(W_RUNS[0], None)
+        load_x(1, [1])
+        load_w(W_RUNS[1], None)
+        nc.sync.dma_start(gate_rows[KEPT][:], gate[0:P, KEPT:OWN])
+        load_x(1, [2])
+        load_w(W_RUNS[2], AT_RAW2)
+        load_x(1, [3])
+        load_w(W_RUNS[3], None)
+        load_x(2, [0])
+        load_w(W_RUNS[4], AT_RAW4)
+        load_x(2, [1, 2, 3])
+        nc.sync.dma_start(gate_rows[C][:], gate[0:P, C:FINAL])
         nc.sync.dma_start(b_sb[:], b)
         nc.sync.dma_start(pos1_sb[:], pos1)
         nc.sync.dma_start(pos2_sb[:], pos2)
@@ -124,68 +117,71 @@ def tile_moe_pre_lin_bias_kernel(tc, xT, w, b, gate, offs, pos1, pos2, out):
             return tile[:].indirect(lst[:, lo // PER_COL : hi // PER_COL])
 
         picked = {}
+        rounds = {}
+        scales = {}
 
-        def pick(g, lo, hi, buffer):
-            picked[g, lo] = turns.tile([P, PACK, hi - lo], F32, name=buffer, align_bytes=64)
+        def holder(tiles, kind, lo):
+            return max(a for k, a in tiles if k == kind and a <= lo)
+
+        def gathered(g, lo, hi):
+            first = holder(picked, g, lo)
+            return picked[g, first][:, :, lo - first : hi - first]
+
+        def rounded(kind, lo, hi):
+            first = holder(rounds, kind, lo)
+            return rounds[kind, first][:, (lo - first) * PACK : (hi - first) * PACK]
+
+        def scaled(kind, lo, hi):
+            first = holder(scales, kind, lo)
+            return scales[kind, first][:, lo - first : hi - first]
+
+        def room(kind, lo, hi, where):
+            rounds[kind, lo] = place([P, (hi - lo) * PACK], BF16, f"round_{kind}_{lo}", where)
+
+        def pick(g, lo, hi, where):
+            picked[g, lo] = place([P, PACK, hi - lo], F32, f"picked{g}_{lo}", where)
             for t in range(PACK):
                 nc.scalar.activation(picked[g, lo][:, t, :], listed(win[g, t], offs_sb, lo, hi), COPY)
 
         def own():
-            picked[0, 0] = turns.tile([P, PACK, OWN], F32, name="b", align_bytes=64)
-            for t in range(PACK):
+            picked[0, 0] = place([P, PACK, OWN], F32, "picked_own", AT_OWN)
+            for t in range(PACK - 1):
                 nc.vector.tensor_copy(picked[0, 0][:, t, :], listed(win[0, t], offs_sb, 0, OWN))
+            for lo, hi in ((0, BANK), (BANK, OWN)):
+                nc.vector.tensor_copy(picked[0, 0][:, PACK - 1, lo:hi], listed(win[0, PACK - 1], offs_sb, lo, hi))
 
-        def columns(tiles, kind, g, lo, hi, per=1):
-            first = max(a for k, p, a in tiles if (k, p) == (kind, g) and a <= lo)
-            return tiles[kind, g, first][:, (lo - first) * per : (hi - first) * per]
-
-        def rounded(kind, g, lo, hi):
-            return columns(rounds, kind, g, lo, hi, PACK)
-
-        def weigh(g, first, last, cuts=()):
-            cuts = sorted({first, last, *cuts, *[c for c in range(BANK, S, BANK) if first < c < last]})
+        def weigh(g, first, last):
+            cuts = sorted({first, last, *[c for c in range(BANK, S, BANK) if first < c < last]})
             for lo, hi in zip(cuts, cuts[1:]):
                 j = lo // BANK
                 nc.vector.tensor_tensor(
-                    rounded("x", g, lo, hi).rearrange("p (c i t) -> p c t i", i=2, t=PACK),
-                    picked[g, first][:, :, lo - first : hi - first].rearrange("p t (c i) -> p c t i", i=2),
+                    rounded(g, lo, hi).rearrange("p (c i t) -> p c t i", i=2, t=PACK),
+                    gathered(g, lo, hi).rearrange("p t (c i) -> p c t i", i=2),
                     spread[j][:, lo - j * BANK : hi - j * BANK]
                     .rearrange("p (c o i) -> p c o i", o=1, i=2)
                     .to_broadcast([P, (hi - lo) // 2, PACK, 2]),
                     MULT,
                 )
 
-        rounds["x", 0, 0] = turns.tile([P, S * PACK], BF16, name="x_round0", align_bytes=64)
-        pick(*UNITS[0])
+        def weigh_beside(g, lo, hi):
+            first = max(a for a in gate_rows if a <= lo)
+            nc.gpsimd.tensor_tensor(
+                rounded(g, lo, hi).rearrange("p (c i t) -> p c t i", i=2, t=PACK),
+                gathered(g, lo, hi).rearrange("p t (c i) -> p c t i", i=2),
+                gate_rows[first][:, lo - first : hi - first]
+                .rearrange("p (c o i) -> p c o i", o=1, i=2)
+                .to_broadcast([P, (hi - lo) // 2, PACK, 2]),
+                MULT,
+            )
 
         def round_w(run):
             first, end = run
-            nc.gpsimd.tensor_scalar(
-                rounded("w", 0, first * N, end * N).rearrange("p (e n t) -> p e n t", n=N, t=PACK),
-                w_raw[run][:].rearrange("p e t n -> p e n t"),
-                1.0,
-                0.0,
-                MULT,
-                ADD,
+            nc.gpsimd.tensor_copy(
+                rounded("w", first * N, end * N).rearrange("p (e c i t) -> p e c t i", c=N // 2, i=2, t=PACK),
+                w_raw[run][:].rearrange("p e t (c i) -> p e c t i", i=2),
             )
 
-        def weigh_beside(first, lo, hi):
-            nc.gpsimd.tensor_tensor(
-                rounded("x", 0, lo, hi).rearrange("p (s t) -> p s t", t=PACK),
-                picked[0, first][:, :, lo - first : hi - first].rearrange("p t s -> p s t"),
-                gate_rows[:, lo - KEPT : hi - KEPT].rearrange("p (s o) -> p s o", o=1).to_broadcast([P, hi - lo, PACK]),
-                MULT,
-            )
-
-        own()
-        round_w(W_RUNS[0])
-        weigh_beside(OWN, OWN, S)
-        round_w(W_RUNS[1])
-        weigh_beside(0, KEPT, OWN)
-        for run in W_RUNS[2:4]:
-            round_w(run)
-
-        done = {}
+        quantised = set()
         passes_done = [0] * len(GROUPS)
         in_bank = [0] * len(BANKS)
 
@@ -195,15 +191,15 @@ def tile_moe_pre_lin_bias_kernel(tc, xT, w, b, gate, offs, pos1, pos2, out):
                 base, end = BANKS[k]
                 members = [m for m in GROUPS if base <= m[0] < end]
                 g = passes_done[i]
-                while g < PASSES and done.get(("x", g), 0) >= hi and done.get(("w", 0), 0) >= (g * E + lo // C + 1) * N:
+                while g < PASSES and {(g, c) for c in range(lo, hi, N)} | {("w", (g * E + lo // C) * N)} <= quantised:
                     j = g * E + lo // C
                     in_bank[k] += 1
                     nc.tensor.matmul_mx(
                         out=acc[k][:, lo - base : hi - base],
-                        lhsT=columns(codes, "w", 0, j * N, (j + 1) * N).bitcast(FP8X4),
-                        lhsT_scale=columns(scales, "w", 0, j * N, (j + 1) * N),
-                        rhs=columns(codes, "x", g, lo, hi).bitcast(FP8X4),
-                        rhs_scale=columns(scales, "x", g, lo, hi),
+                        lhsT=codes["w"][:, j * N : (j + 1) * N].bitcast(FP8X4),
+                        lhsT_scale=scaled("w", j * N, (j + 1) * N),
+                        rhs=codes[g][:, lo:hi].bitcast(FP8X4),
+                        rhs_scale=scaled(g, lo, hi),
                         start=(in_bank[k] == 1),
                         stop=(in_bank[k] == PASSES * len(members)),
                     )
@@ -212,65 +208,72 @@ def tile_moe_pre_lin_bias_kernel(tc, xT, w, b, gate, offs, pos1, pos2, out):
                     if in_bank[k] == PASSES * len(members):
                         for a, z in members:
                             e = a // C
-                            if k == len(BANKS) - 1:
+                            if k >= len(BANKS) - 2:
                                 nc.vector.tensor_scalar(y[:, a:z], acc[k][:], b_sb[:, e : e + 1], None, ADD)
                             else:
                                 nc.scalar.activation(
                                     y[:, a:z], acc[k][:, a - base : z - base], IDENT, bias=b_sb[:, e : e + 1]
                                 )
 
-        free = [0]
-
-        def quantize(kind, g, *ends):
-            first = done.get((kind, g), 0)
-            name = f"{kind}{g}_{first}"
-            width = ends[-1] - first
-            codes[kind, g, first] = keep.tile([P, width], U32, name=f"codes_{name}", align_bytes=64)
-            scales[kind, g, first] = laid.tile([P, width], U8, name=f"scales_{name}", align_bytes=64, offset=free[0])
-            free[0] += width
-            for hi in ends:
-                lo = done.get((kind, g), 0)
-                nc.vector.quantize_mx(
-                    out=columns(codes, kind, g, lo, hi).bitcast(FP8X4),
-                    scales=columns(scales, kind, g, lo, hi),
-                    in_=rounded(kind, g, lo, hi),
-                )
-                done[kind, g] = hi
+        def quantize(kind, lo, hi, where):
+            scales[kind, lo] = place([P, hi - lo], U8, f"scales_{kind}_{lo}", where)
+            nc.vector.quantize_mx(
+                out=codes[kind][:, lo:hi].bitcast(FP8X4), scales=scaled(kind, lo, hi), in_=rounded(kind, lo, hi)
+            )
+            for c in range(lo, hi, N):
+                quantised.add((kind, c))
             multiply_ready()
 
-        rounds["x", 1, 0] = keep.tile([P, FIRST * PACK], BF16, name="x_round1", align_bytes=64)
-        pick(*UNITS[1])
+        room(0, 0, S, AT_X0)
+        room("w", 0, 6 * N, AT_W0)
+        room("w", 6 * N, 10 * N, None)
+
+        pick(0, OWN, S, None)
+        own()
+        weigh_beside(0, OWN, S)
+        round_w(W_RUNS[0])
+        round_w(W_RUNS[1])
+        weigh_beside(0, KEPT, OWN)
+        round_w(W_RUNS[2])
+        pick(1, 0, S, AT_ALL)
         weigh(0, 0, KEPT)
-        pick(*UNITS[2])
-        weigh(1, 0, FIRST)
-        pick(*UNITS[3])
-        quantize("w", 0, 8 * N, 10 * N)
-        pick(*UNITS[4])
-        quantize("x", 0, 1024, 1536)
-        rounds["w", 0, 10 * N] = turns.tile([P, 6 * N * PACK], BF16, name="x_round0", align_bytes=64)
+        pick(2, 512, S, AT_OWN)
+
+        quantize(0, 0, 1024, AT_RAW2 + 2 * KIB)
+        quantize(0, 1024, S, AT_RAW2 + 3 * KIB)
+        quantize("w", 0, 4 * N, None)
+        quantize("w", 4 * N, 6 * N, None)
+        quantize("w", 6 * N, 10 * N, None)
+
+        room("w", 10 * N, 18 * N, AT_W0)
+        room(1, 0, 1024, AT_RAW2 - 6 * KIB)
+        room(1, 1024, S, AT_RAW2 + 4 * KIB)
+        round_w(W_RUNS[3])
+        weigh_beside(1, MID, S)
         round_w(W_RUNS[4])
-        free[0] = HOLDS[W_RUNS[4]]
-        held = laid.tile([P, (S - FIRST + 512) * PACK], BF16, name="held", align_bytes=64, offset=2 * BLOCK)
-        rounds["x", 1, FIRST] = held[:, 0 : (S - FIRST) * PACK]
-        rounds["x", 2, 0] = held[:, (S - FIRST) * PACK :]
-        weigh(1, FIRST, S)
-        pick(*UNITS[5])
-        weigh(2, 0, 512)
-        pick(*UNITS[6])
-        quantize("w", 0, 14 * N, 16 * N)
-        rounds["x", 2, 512] = turns.tile([P, (S - 512) * PACK], BF16, name="x_round0", align_bytes=64)
-        quantize("x", 1, 512, FIRST, FIRST + 512, S)
-        quantize("x", 2, 512)
-        rounds["w", 0, 16 * N] = laid.tile([P, 2 * N * PACK], BF16, name="w_last", align_bytes=64, offset=2 * BLOCK)
-        round_w(W_RUNS[5])
-        weigh(2, 512, 1024)
-        quantize("w", 0, 18 * N)
-        quantize("x", 2, 1024)
-        weigh(2, 1024, 1344, [1280])
-        quantize("x", 2, 1280)
-        weigh(2, 1344, 1536, [1408])
-        quantize("x", 2, 1408)
-        quantize("x", 2, 1536)
+        weigh(1, 0, MID)
+        pick(2, 0, 256, AT_ALL)
+        pick(2, 256, 512, AT_ALL + 4 * KIB)
+
+        quantize("w", 10 * N, 18 * N, None)
+        quantize(1, 0, 1024, AT_RAW4)
+        quantize(1, 1024, S, AT_RAW4 + KIB)
+
+        room(2, 512, S, AT_RAW2 - 6 * KIB)
+        weigh_beside(2, LATE, S)
+        weigh(2, 512, LATE)
+        room(2, 0, 256, AT_RAW4 + 2 * KIB)
+        weigh(2, 0, 256)
+        quantize(2, 512, 1024, AT_OWN + 2 * KIB)
+        quantize(2, 1024, S, None)
+        quantize(2, 0, 256, AT_OWN)
+        room(2, 384, 512, AT_OWN + KIB)
+        room(2, 256, 384, AT_RAW2 - 6 * KIB)
+        weigh_beside(2, 256, FINAL)
+        weigh(2, 384, 512)
+        weigh(2, FINAL, 384)
+        quantize(2, 384, 512, None)
+        quantize(2, 256, 384, None)
 
         first = keep.tile([P, T], F32, name="first")
         total = keep.tile([P, T], F32, name="total")

@@ -27,9 +27,9 @@ IDENT = mybir.ActivationFunctionType.Identity
 COPY = mybir.ActivationFunctionType.Copy
 
 OWN = 1152
-KEPT = 1120
-MID = 1488
-LATE = 1216
+KEPT = 1104
+MID = 1472
+LATE = 1200
 FINAL = 304
 GROUPS = [(512, 768), (768, 1024), (1024, 1280), (1280, 1536), (0, 256), (384, 512), (256, 384)]
 BANKS = [(512, 1024), (1024, 1536), (0, 256), (384, 512), (256, 384)]
@@ -166,19 +166,19 @@ def tile_moe_pre_lin_bias_kernel(tc, xT, w, b, gate, offs, pos1, pos2, out):
         def weigh_beside(g, lo, hi):
             first = max(a for a in gate_rows if a <= lo)
             nc.gpsimd.tensor_tensor(
-                rounded(g, lo, hi).rearrange("p (c i t) -> p c t i", i=2, t=PACK),
-                gathered(g, lo, hi).rearrange("p t (c i) -> p c t i", i=2),
+                rounded(g, lo, hi).rearrange("p (c i t) -> p c t i", i=4, t=PACK),
+                gathered(g, lo, hi).rearrange("p t (c i) -> p c t i", i=4),
                 gate_rows[first][:, lo - first : hi - first]
-                .rearrange("p (c o i) -> p c o i", o=1, i=2)
-                .to_broadcast([P, (hi - lo) // 2, PACK, 2]),
+                .rearrange("p (c o i) -> p c o i", o=1, i=4)
+                .to_broadcast([P, (hi - lo) // 4, PACK, 4]),
                 MULT,
             )
 
         def round_w(run):
             first, end = run
             nc.gpsimd.tensor_copy(
-                rounded("w", first * N, end * N).rearrange("p (e c i t) -> p e c t i", c=N // 2, i=2, t=PACK),
-                w_raw[run][:].rearrange("p e t (c i) -> p e c t i", i=2),
+                rounded("w", first * N, end * N).rearrange("p (e c i t) -> p e c t i", c=N // 4, i=4, t=PACK),
+                w_raw[run][:].rearrange("p e t (c i) -> p e c t i", i=4),
             )
 
         quantised = set()

@@ -27,10 +27,10 @@ IDENT = mybir.ActivationFunctionType.Identity
 COPY = mybir.ActivationFunctionType.Copy
 
 OWN = 1152
-KEPT = 1104
-MID = 1472
-LATE = 1200
-FINAL = 304
+KEPT = 1088
+MID = 1456
+LATE = 1184
+FINAL = 320
 GROUPS = [(512, 768), (768, 1024), (1024, 1280), (1280, 1536), (0, 256), (384, 512), (256, 384)]
 BANKS = [(512, 1024), (1024, 1536), (0, 256), (384, 512), (256, 384)]
 OUT = [(0, 256), (256, 512), (512, 768)]

@@ -26,8 +26,8 @@ ADD = mybir.AluOpType.add
 IDENT = mybir.ActivationFunctionType.Identity
 COPY = mybir.ActivationFunctionType.Copy
 
-OWN = 1152
-KEPT = 1088
+OWN = 1184
+KEPT = 1056
 MID = 1456
 LATE = 1184
 FINAL = 320

from contextlib import ExitStack

import concourse.mybir as mybir
from concourse.masks import make_identity

K, T, E, C, N = 1536, 768, 6, 256, 128
S = E * C
P = 128
PACK = 4
K_PASS = P * PACK
PASSES = K // K_PASS
PER_COL = 16
BANK = 512

FLOPS = 2 * K * S * N
BYTES = 4 * (K * T + E * K * N + N * E + S + N * T) + 2 * P * (S + 2 * T) // PER_COL

F32 = mybir.dt.float32
BF16 = mybir.dt.bfloat16
U32 = mybir.dt.uint32
U16 = mybir.dt.uint16
U8 = mybir.dt.uint8
FP8X4 = mybir.dt.float8_e4m3fn_x4
MULT = mybir.AluOpType.mult
ADD = mybir.AluOpType.add
IDENT = mybir.ActivationFunctionType.Identity
COPY = mybir.ActivationFunctionType.Copy

OWN = 1184
KEPT = 1056
MID = 1456
LATE = 1184
FINAL = 320
GROUPS = [(512, 768), (768, 1024), (1024, 1280), (1280, 1536), (0, 256), (384, 512), (256, 384)]
BANKS = [(512, 1024), (1024, 1536), (0, 256), (384, 512), (256, 384)]
OUT = [(0, 256), (256, 512), (512, 768)]
W_EXPERTS = 2
W_RUNS = [(0, 2), (2, 6), (6, 10), (10, 14), (14, 18)]
WINDOW = [OWN + PER_COL, S + PER_COL, 1024 + PER_COL]
KIB = 1024
AT_X0, AT_RAW2, AT_W0, AT_RAW4, AT_OWN, AT_ALL = 0, 18 * KIB, 26 * KIB, 34 * KIB, 42 * KIB, 61 * KIB


def tile_moe_pre_lin_bias_kernel(tc, xT, w, b, gate, offs, pos1, pos2, out):
    nc = tc.nc
    with ExitStack() as ctx:
        keep = ctx.enter_context(tc.tile_pool(name="keep", bufs=1))
        laid = ctx.enter_context(tc.tile_pool(name="laid", bufs=1))
        psum = ctx.enter_context(tc.psum_pool(name="psum", bufs=1))

        offs_sb = keep.tile([P, S // PER_COL], U16, name="offs_sb")
        pos1_sb = keep.tile([P, T // PER_COL], U16, name="pos1_sb")
        pos2_sb = keep.tile([P, T // PER_COL], U16, name="pos2_sb")
        b_sb = keep.tile([P, E], F32, name="b_sb")
        gate_sb = keep.tile([P, S // BANK, BANK // P], F32, name="gate_sb")
        gate_rows = {lo: keep.tile([P, hi - lo], F32, name=f"gate_rows{lo}") for lo, hi in ((KEPT, OWN), (OWN, S), (C, FINAL))}
        ident = keep.tile([P, P], F32, name="ident")
        y = keep.tile([P, S], F32, name="y")
        spread = [psum.tile([P, BANK], F32, name=f"spread{j}") for j in range(S // BANK)]
        acc = [psum.tile([P, hi - lo], F32, name=f"acc{i}") for i, (lo, hi) in enumerate(BANKS)]
        codes = {g: keep.tile([P, S], U32, name=f"codes_x{g}", align_bytes=64) for g in range(PASSES)}
        codes["w"] = keep.tile([P, PASSES * E * N], U32, name="codes_w", align_bytes=64)

        def place(shape, dtype, name, where):
            if where is None:
                return keep.tile(shape, dtype, name=name, align_bytes=64)
            return laid.tile(shape, dtype, name=name, align_bytes=64, offset=where)

        x_rows = xT.rearrange("(g p t) x -> g t p x", g=PASSES, t=PACK)
        w_rows = w.rearrange("e (g p t) n -> g p e t n", g=PASSES, t=PACK)
        win = {}
        w_raw = {}

        def load_x(g, planes):
            for t in planes:
                win[g, t] = keep.tile([P, WINDOW[g]], F32, name=f"win{g}_{t}")
                nc.sync.dma_start(win[g, t][:, 0:T], x_rows[g, t])

        def load_w(run, where):
            first, end = run
            w_raw[run] = place([P, end - first, PACK, N], F32, f"w_raw{first}", where)
            for lo in range(first, end, W_EXPERTS):
                hi = lo + W_EXPERTS
                nc.sync.dma_start(w_raw[run][:, lo - first : hi - first], w_rows[lo // E][:, lo % E : lo % E + W_EXPERTS])

        warm = keep.tile([P, 2], F32, name="warm")
        nc.vector.memset(warm[:, 0:1], 0.0)
        nc.scalar.activation(warm[:, 1:2], warm[:, 0:1], IDENT)

        nc.sync.dma_start(offs_sb[:], offs)
        load_x(0, range(PACK))
        load_x(1, [0])
        nc.sync.dma_start(gate_rows[OWN][:], gate[0:P, OWN:S])
        nc.sync.dma_start(gate_sb[:], gate[0].rearrange("(j q r) -> q j r", q=P, r=BANK // P))
        load_w(W_RUNS[0], None)
        load_x(1, [1])
        load_w(W_RUNS[1], None)
        nc.sync.dma_start(gate_rows[KEPT][:], gate[0:P, KEPT:OWN])
        load_x(1, [2])
        load_w(W_RUNS[2], AT_RAW2)
        load_x(1, [3])
        load_w(W_RUNS[3], None)
        load_x(2, [0])
        load_w(W_RUNS[4], AT_RAW4)
        load_x(2, [1, 2, 3])
        nc.sync.dma_start(gate_rows[C][:], gate[0:P, C:FINAL])
        nc.sync.dma_start(b_sb[:], b)
        nc.sync.dma_start(pos1_sb[:], pos1)
        nc.sync.dma_start(pos2_sb[:], pos2)

        make_identity(nc, ident[:])
        for j in range(S // BANK):
            for r in range(BANK // P):
                nc.tensor.transpose(spread[j][:, r :: BANK // P], gate_sb[:, j, r : r + 1].to_broadcast([P, P]), ident[:])

        def listed(tile, lst, lo, hi):
            return tile[:].indirect(lst[:, lo // PER_COL : hi // PER_COL])

        picked = {}
        rounds = {}
        scales = {}

        def holder(tiles, kind, lo):
            return max(a for k, a in tiles if k == kind and a <= lo)

        def gathered(g, lo, hi):
            first = holder(picked, g, lo)
            return picked[g, first][:, :, lo - first : hi - first]

        def rounded(kind, lo, hi):
            first = holder(rounds, kind, lo)
            return rounds[kind, first][:, (lo - first) * PACK : (hi - first) * PACK]

        def scaled(kind, lo, hi):
            first = holder(scales, kind, lo)
            return scales[kind, first][:, lo - first : hi - first]

        def room(kind, lo, hi, where):
            rounds[kind, lo] = place([P, (hi - lo) * PACK], BF16, f"round_{kind}_{lo}", where)

        def pick(g, lo, hi, where):
            picked[g, lo] = place([P, PACK, hi - lo], F32, f"picked{g}_{lo}", where)
            for t in range(PACK):
                nc.scalar.activation(picked[g, lo][:, t, :], listed(win[g, t], offs_sb, lo, hi), COPY)

        def own():
            picked[0, 0] = place([P, PACK, OWN], F32, "picked_own", AT_OWN)
            for t in range(PACK - 1):
                nc.vector.tensor_copy(picked[0, 0][:, t, :], listed(win[0, t], offs_sb, 0, OWN))
            for lo, hi in ((0, BANK), (BANK, OWN)):
                nc.vector.tensor_copy(picked[0, 0][:, PACK - 1, lo:hi], listed(win[0, PACK - 1], offs_sb, lo, hi))

        def weigh(g, first, last):
            cuts = sorted({first, last, *[c for c in range(BANK, S, BANK) if first < c < last]})
            for lo, hi in zip(cuts, cuts[1:]):
                j = lo // BANK
                nc.vector.tensor_tensor(
                    rounded(g, lo, hi).rearrange("p (c i t) -> p c t i", i=2, t=PACK),
                    gathered(g, lo, hi).rearrange("p t (c i) -> p c t i", i=2),
                    spread[j][:, lo - j * BANK : hi - j * BANK]
                    .rearrange("p (c o i) -> p c o i", o=1, i=2)
                    .to_broadcast([P, (hi - lo) // 2, PACK, 2]),
                    MULT,
                )

        def weigh_beside(g, lo, hi):
            first = max(a for a in gate_rows if a <= lo)
            nc.gpsimd.tensor_tensor(
                rounded(g, lo, hi).rearrange("p (c i t) -> p c t i", i=4, t=PACK),
                gathered(g, lo, hi).rearrange("p t (c i) -> p c t i", i=4),
                gate_rows[first][:, lo - first : hi - first]
                .rearrange("p (c o i) -> p c o i", o=1, i=4)
                .to_broadcast([P, (hi - lo) // 4, PACK, 4]),
                MULT,
            )

        def round_w(run):
            first, end = run
            nc.gpsimd.tensor_copy(
                rounded("w", first * N, end * N).rearrange("p (e c i t) -> p e c t i", c=N // 4, i=4, t=PACK),
                w_raw[run][:].rearrange("p e t (c i) -> p e c t i", i=4),
            )

        quantised = set()
        passes_done = [0] * len(GROUPS)
        in_bank = [0] * len(BANKS)

        def multiply_ready():
            for i, (lo, hi) in enumerate(GROUPS):
                k = [n for n, (a, z) in enumerate(BANKS) if a <= lo < z][0]
                base, end = BANKS[k]
                members = [m for m in GROUPS if base <= m[0] < end]
                g = passes_done[i]
                while g < PASSES and {(g, c) for c in range(lo, hi, N)} | {("w", (g * E + lo // C) * N)} <= quantised:
                    j = g * E + lo // C
                    in_bank[k] += 1
                    nc.tensor.matmul_mx(
                        out=acc[k][:, lo - base : hi - base],
                        lhsT=codes["w"][:, j * N : (j + 1) * N].bitcast(FP8X4),
                        lhsT_scale=scaled("w", j * N, (j + 1) * N),
                        rhs=codes[g][:, lo:hi].bitcast(FP8X4),
                        rhs_scale=scaled(g, lo, hi),
                        start=(in_bank[k] == 1),
                        stop=(in_bank[k] == PASSES * len(members)),
                    )
                    g += 1
                    passes_done[i] = g
                    if in_bank[k] == PASSES * len(members):
                        for a, z in members:
                            e = a // C
                            if k >= len(BANKS) - 2:
                                nc.vector.tensor_scalar(y[:, a:z], acc[k][:], b_sb[:, e : e + 1], None, ADD)
                            else:
                                nc.scalar.activation(
                                    y[:, a:z], acc[k][:, a - base : z - base], IDENT, bias=b_sb[:, e : e + 1]
                                )

        def quantize(kind, lo, hi, where):
            scales[kind, lo] = place([P, hi - lo], U8, f"scales_{kind}_{lo}", where)
            nc.vector.quantize_mx(
                out=codes[kind][:, lo:hi].bitcast(FP8X4), scales=scaled(kind, lo, hi), in_=rounded(kind, lo, hi)
            )
            for c in range(lo, hi, N):
                quantised.add((kind, c))
            multiply_ready()

        room(0, 0, S, AT_X0)
        room("w", 0, 6 * N, AT_W0)
        room("w", 6 * N, 10 * N, None)

        pick(0, OWN, S, None)
        own()
        weigh_beside(0, OWN, S)
        round_w(W_RUNS[0])
        round_w(W_RUNS[1])
        weigh_beside(0, KEPT, OWN)
        round_w(W_RUNS[2])
        pick(1, 0, S, AT_ALL)
        weigh(0, 0, KEPT)
        pick(2, 512, S, AT_OWN)

        quantize(0, 0, 1024, AT_RAW2 + 2 * KIB)
        quantize(0, 1024, S, AT_RAW2 + 3 * KIB)
        quantize("w", 0, 4 * N, None)
        quantize("w", 4 * N, 6 * N, None)
        quantize("w", 6 * N, 10 * N, None)

        room("w", 10 * N, 18 * N, AT_W0)
        room(1, 0, 1024, AT_RAW2 - 6 * KIB)
        room(1, 1024, S, AT_RAW2 + 4 * KIB)
        round_w(W_RUNS[3])
        weigh_beside(1, MID, S)
        round_w(W_RUNS[4])
        weigh(1, 0, MID)
        pick(2, 0, 256, AT_ALL)
        pick(2, 256, 512, AT_ALL + 4 * KIB)

        quantize("w", 10 * N, 18 * N, None)
        quantize(1, 0, 1024, AT_RAW4)
        quantize(1, 1024, S, AT_RAW4 + KIB)

        room(2, 512, S, AT_RAW2 - 6 * KIB)
        weigh_beside(2, LATE, S)
        weigh(2, 512, LATE)
        room(2, 0, 256, AT_RAW4 + 2 * KIB)
        weigh(2, 0, 256)
        quantize(2, 512, 1024, AT_OWN + 2 * KIB)
        quantize(2, 1024, S, None)
        quantize(2, 0, 256, AT_OWN)
        room(2, 384, 512, AT_OWN + KIB)
        room(2, 256, 384, AT_RAW2 - 6 * KIB)
        weigh_beside(2, 256, FINAL)
        weigh(2, 384, 512)
        weigh(2, FINAL, 384)
        quantize(2, 384, 512, None)
        quantize(2, 256, 384, None)

        first = keep.tile([P, T], F32, name="first")
        total = keep.tile([P, T], F32, name="total")
        last_lo, last_hi = OUT[-1]
        second = keep.tile([P, last_hi - last_lo], F32, name="second")
        nc.vector.tensor_copy(second[:], listed(y, pos2_sb, last_lo, last_hi))
        for lo, hi in OUT:
            nc.scalar.activation(first[:, lo:hi], listed(y, pos1_sb, lo, hi), COPY)
        for lo, hi in OUT[:-1]:
            nc.vector.tensor_tensor(total[:, lo:hi], listed(y, pos2_sb, lo, hi), first[:, lo:hi], ADD)
            nc.sync.dma_start(out[:, lo:hi], total[:, lo:hi])
        nc.vector.tensor_tensor(total[:, last_lo:last_hi], second[:], first[:, last_lo:last_hi], ADD)
        nc.sync.dma_start(out[:, last_lo:last_hi], total[:, last_lo:last_hi])
